import numpy as np
import ml_dtypes


def mxq(x, axis, fmt="e4m3"):
    dtype, down = {"e4m3": (ml_dtypes.float8_e4m3fn, 7), "e5m2": (ml_dtypes.float8_e5m2, 14)}[fmt]
    v = np.moveaxis(np.asarray(x, np.float32).astype(ml_dtypes.bfloat16).astype(np.float64), axis, -1)
    blocks = v.reshape(v.shape[:-1] + (-1, 32))
    amax = np.abs(blocks).max(-1, keepdims=True)
    byte = np.maximum(np.where(amax > 0, np.frexp(amax)[1] - 1 + 127, 0) - down, 1)
    scale = np.exp2(byte - 127.0)
    codes = (blocks / scale).astype(np.float32).astype(dtype).astype(np.float64)
    return np.moveaxis((codes * scale).reshape(v.shape), -1, axis)


WIDE = False


def mx_kscale(k):
    if not WIDE:
        return np.ones(k)
    levels = np.array([10, -10, 5, -5, 0])
    if k % 512:
        return np.exp2(np.random.permutation(np.resize(levels, k // 32))).repeat(32)
    a = np.empty((k // 512, 16))
    for p in range(k // 512):
        a[p, :8] = np.random.permutation(np.resize(levels, 8))
        for g in range(8):
            far = levels[np.abs(levels - a[p, g]) >= 10]
            a[p, g + 8] = far[np.random.randint(len(far))]
    return np.exp2(a.ravel()).repeat(32)


def f64(x):
    return np.asarray(x).astype(np.float64)


def striped(idx):
    return np.tile(idx.reshape(-1, 16).T, (8, 1)).astype(np.uint16)


def unstriped(offs):
    return offs[:16].T.reshape(-1).astype(np.int64)


def pack_weight(w):
    k, n = w.shape
    w = f64(np.asarray(w, np.float32).astype(ml_dtypes.bfloat16)).reshape(k // 32, 32, n)
    amax = np.abs(w).max(1)
    byte = np.clip(np.where(amax > 0, np.frexp(amax)[1] - 1 + 127 - 7, 1), 1, 254)
    scaled = (w * np.exp2(127.0 - byte)[:, None, :]).reshape(k, n).astype(np.float32)
    words = np.ascontiguousarray(scaled.reshape(k // 512, 128, 4, n).transpose(0, 1, 3, 2)).astype(ml_dtypes.float8_e4m3fn).view(np.uint8)
    return words, np.ascontiguousarray(byte.astype(np.uint8).reshape(k // 512, 16, n))


def unpack_weight(words, scales):
    g, p, n, _ = words.shape
    vals = np.ascontiguousarray(words).view(ml_dtypes.float8_e4m3fn).astype(np.float64) * np.repeat(np.exp2(scales.astype(np.float64) - 127.0), 8, axis=1)[..., None]
    return vals.transpose(0, 1, 3, 2).reshape(g * 512, n)


K, T, S, D, H, N, V = 512, 2048, 1024, 2, 512, 128, 512


def setup_inputs():
    n = np.random.standard_normal
    s = mx_kscale(K)[:, None]
    u = mx_kscale(H)
    packed_xT = pack_weight(n((K, T)) * s)
    return {
        "x_words": packed_xT[0],
        "x_scales": packed_xT[1],
        "w1": (n((K, H)) / np.sqrt(K) / s * u).astype(np.float32),
        "t1": (n((H, N)) / np.sqrt(4 * H) / u[:, None]).astype(np.float32),
        "t2": (n((H, N)) / np.sqrt(4 * H) / u[:, None]).astype(np.float32),
        "t3": (n((H, N)) / np.sqrt(4 * H) / u[:, None]).astype(np.float32),
        "w2": (n((K, N)) / np.sqrt(4 * K) / s).astype(np.float32),
        "bias": (0.5 * n((N, 1))).astype(np.float32),
        "offs": striped(np.random.permutation(T)[:S]),
        "far1": striped(np.random.permutation(V)),
        "far2": striped(np.random.permutation(V)),
        "far3": striped(np.random.permutation(V)),
        "close": striped(np.random.permutation(T)[:V]),
    }


def reference(x_words, x_scales, w1, t1, t2, t3, w2, bias, offs, far1, far2, far3, close):
    xq = unpack_weight(x_words, x_scales)[:, unstriped(offs)]
    y = mxq(f64(w1), 0, "e4m3").T @ xq
    h = y.reshape(len(y), -1, D).sum(axis=2)
    m0 = h[:, unstriped(far1)]
    m1 = h[:, unstriped(far2)]
    m2 = h[:, unstriped(far3)]
    x_close = unpack_weight(x_words, x_scales)[:, unstriped(close)]
    return np.tanh((mxq(f64(t1), 0, "e4m3").T @ mxq(m0, 0, "e4m3") + mxq(f64(t2), 0, "e4m3").T @ mxq(m1, 0, "e4m3") + mxq(f64(t3), 0, "e4m3").T @ mxq(m2, 0, "e4m3") + mxq(f64(w2), 0, "e4m3").T @ x_close) + f64(bias))

@@ -1,0 +1,189 @@
+from contextlib import ExitStack
+
+import concourse.mybir as mybir
+
+K, T, S, D, H, N, V = 512, 2048, 1024, 2, 512, 128, 512
+FLOPS = 2 * K * H * S + 3 * 2 * H * N * V + 2 * K * N * V
+
+F32 = mybir.dt.float32
+BF16 = mybir.dt.bfloat16
+I32 = mybir.dt.int32
+U32 = mybir.dt.uint32
+U16 = mybir.dt.uint16
+U8 = mybir.dt.uint8
+FP8X4 = mybir.dt.float8_e4m3fn_x4
+TANH = mybir.ActivationFunctionType.Tanh
+
+P = 128
+PACK = 4
+GROUP = 16
+SPARE = 192
+CHUNKS = ((0, 256), (256, 384), (384, 512))
+
+
+def tile_picked_yfmm_tanh_p_kernel(
+    tc, x_words, x_scales, w1, t1, t2, t3, w2, bias, offs, far1, far2, far3, close, out
+):
+    nc = tc.nc
+    with ExitStack() as ctx:
+        keep = ctx.enter_context(tc.tile_pool(name="keep", bufs=1))
+        psum = ctx.enter_context(tc.psum_pool(name="psum", bufs=1))
+
+        def load_list(src, name):
+            tile = keep.tile(list(src.shape), U16, name=name)
+            nc.sync.dma_start(tile[:], src)
+            return tile
+
+        def entries(tile, lo, hi):
+            return tile[:, lo // GROUP : hi // GROUP]
+
+        x_bytes = keep.tile([P, T], U8, name="x_bytes", align_bytes=64)
+        nc.vector.memset(x_bytes[:].bitcast(I32), 0)
+        offs_sb = load_list(offs, "offs_sb")
+        far1_sb = load_list(far1, "far1_sb")
+        close_sb = load_list(close, "close_sb")
+        for q in range(4):
+            nc.sync.dma_start(
+                x_bytes[32 * q : 32 * q + 4, :].bitcast(I32), x_scales[0, 4 * q : 4 * q + 4, :].bitcast(I32)
+            )
+        x_table = keep.tile([P, T], I32, name="x_table", align_bytes=64)
+        nc.sync.dma_start(x_table[:], x_words[0].rearrange("p c r -> p (c r)").bitcast(I32))
+
+        w1_rows = w1.rearrange("(p j) c -> p j c", j=PACK)
+        w1_raw = []
+        for half in range(2):
+            raw = keep.tile([P, PACK, H // 2], F32, name="w1_raw%d" % half, tag="w1_raw%d" % half, align_bytes=64)
+            nc.sync.dma_start(raw[:], w1_rows[:, :, half * (H // 2) : (half + 1) * (H // 2)])
+            w1_raw.append(raw)
+
+        small_raw = []
+        for i, mat in enumerate((w2, t1, t2, t3)):
+            raw = keep.tile([P, PACK, N], F32, name="small_raw%d" % i)
+            nc.sync.dma_start(raw[:], mat.rearrange("(p j) n -> p j n", j=PACK))
+            small_raw.append(raw)
+        far2_sb = load_list(far2, "far2_sb")
+        far3_sb = load_list(far3, "far3_sb")
+        bias_sb = keep.tile([P, 1], F32, name="bias_sb")
+        nc.sync.dma_start(bias_sb[:], bias)
+
+        h = keep.tile([P, PACK * V + SPARE], F32, name="h", align_bytes=64)
+        nc.gpsimd.memset(h[:, PACK * V :], 0.0)
+
+        warm = keep.tile([P, 1], F32, name="warm")
+        nc.scalar.activation(warm[:], h[:, PACK * V : PACK * V + 1], TANH)
+
+        pick_bytes = keep.tile([P, S], U8, name="pick_bytes", align_bytes=64)
+        nc.vector.tensor_copy(pick_bytes[:], x_bytes[:].indirect(offs_sb[:]))
+        pair_bytes = keep.tile([P, D, V], U8, name="pair_bytes", align_bytes=64)
+        nc.vector.tensor_copy(pair_bytes[:], pick_bytes[:].rearrange("p (v d) -> p d v", d=D))
+        pair_words = keep.tile([P, D, V], U32, name="pair_words", align_bytes=64)
+        nc.vector.tensor_copy(
+            pair_words[:].rearrange("p d v -> p v d"), x_table[:].bitcast(U32).indirect(offs_sb[:])
+        )
+
+        w1_bf = [keep.tile([P, 2, P, PACK], BF16, name="w1_bf%d" % u, tag="w1_bf%d" % u, align_bytes=64) for u in range(2)]
+        for half in range(2):
+            ms = slice(half * (P // 2), (half + 1) * (P // 2))
+            src = w1_raw[half][:].rearrange("p j (m t) -> p m j t", t=PACK)
+            for u in range(2):
+                nc.scalar.copy(w1_bf[u][:, :, ms, :].rearrange("p t m j -> p m j t"), src[:, :, :, 2 * u : 2 * u + 2])
+        w1_codes = []
+        w1_scales = []
+        for u in range(2):
+            codes = keep.tile([P, 2 * P], U32, name="w1_codes%d" % u, align_bytes=64)
+            scales = keep.tile([P, 2 * P], U8, name="w1_scales%d" % u, align_bytes=64)
+            nc.vector.quantize_mx(
+                out=codes[:].bitcast(FP8X4), scales=scales[:], in_=w1_bf[u][:].rearrange("p t m j -> p (t m j)")
+            )
+            w1_codes.append(codes)
+            w1_scales.append(scales)
+
+        for t in range(PACK):
+            bank = psum.tile([P, V], F32, name="h_bank%d" % t)
+            cols = slice((t % 2) * P, (t % 2 + 1) * P)
+            for d in range(D):
+                nc.tensor.matmul_mx(
+                    out=bank[:],
+                    lhsT=w1_codes[t // 2][:, cols].bitcast(FP8X4),
+                    lhsT_scale=w1_scales[t // 2][:, cols],
+                    rhs=pair_words[:, d, :].bitcast(FP8X4),
+                    rhs_scale=pair_bytes[:, d, :],
+                    start=(d == 0),
+                    stop=(d == D - 1),
+                )
+            nc.scalar.copy(h[:, t * V : (t + 1) * V], bank[:])
+
+        close_bytes = keep.tile([P, V], U8, name="close_bytes", tag="w1_raw1", align_bytes=64)
+        nc.vector.tensor_copy(close_bytes[:], x_bytes[:].indirect(close_sb[:]))
+        close_words = keep.tile([P, V], U32, name="close_words", tag="w1_bf1", align_bytes=64)
+        nc.vector.tensor_copy(close_words[:], x_table[:].bitcast(U32).indirect(close_sb[:]))
+
+        small_bf = keep.tile([P, 4, N, PACK], BF16, name="small_bf", align_bytes=64)
+        for i in range(4):
+            nc.scalar.copy(
+                small_bf[:, i].rearrange("p (c e) j -> p c j e", e=4),
+                small_raw[i][:].rearrange("p j (c e) -> p c j e", e=4),
+            )
+        small_codes = keep.tile([P, 4 * N], U32, name="small_codes", align_bytes=64)
+        small_scales = keep.tile([P, 4 * N], U8, name="small_scales", align_bytes=64)
+        nc.vector.quantize_mx(
+            out=small_codes[:].bitcast(FP8X4), scales=small_scales[:], in_=small_bf[:].rearrange("p i n j -> p (i n j)")
+        )
+
+        banks = [psum.tile([P, hi - lo], F32, name="out_bank%d" % c) for c, (lo, hi) in enumerate(CHUNKS)]
+
+        def product(i, c, codes, scales):
+            nc.tensor.matmul_mx(
+                out=banks[c][:],
+                lhsT=small_codes[:, i * N : (i + 1) * N].bitcast(FP8X4),
+                lhsT_scale=small_scales[:, i * N : (i + 1) * N],
+                rhs=codes.bitcast(FP8X4),
+                rhs_scale=scales,
+                start=(i == 0),
+                stop=(i == 3),
+            )
+
+        def weave_and_quantize(fetched, width, name):
+            woven = keep.tile([P, width, PACK], BF16, name=name + "_bf", align_bytes=64)
+            nc.scalar.copy(
+                woven[:].rearrange("p (c e) t -> p c t e", e=4), fetched.rearrange("p t (c e) -> p c t e", e=4)
+            )
+            codes = keep.tile([P, width], U32, name=name + "_codes", align_bytes=64)
+            scales = keep.tile([P, width], U8, name=name + "_scales", align_bytes=64)
+            nc.vector.quantize_mx(
+                out=codes[:].bitcast(FP8X4), scales=scales[:], in_=woven[:].rearrange("p c t -> p (c t)")
+            )
+            return codes, scales
+
+        for c, (lo, hi) in enumerate(CHUNKS):
+            product(0, c, close_words[:, lo:hi], close_bytes[:, lo:hi])
+
+        m0 = keep.tile([P, PACK, V], F32, name="m0", tag="stage_a", align_bytes=64)
+        for t in range(PACK):
+            for lo in (0, V // 2):
+                nc.vector.tensor_copy(
+                    m0[:, t, lo : lo + V // 2], h[:, t * V : (t + 1) * V].indirect(entries(far1_sb, lo, lo + V // 2))
+                )
+        m1 = keep.tile([P, PACK, V], F32, name="m1", align_bytes=64)
+        for t in range(PACK):
+            nc.vector.tensor_copy(m1[:, t, :], h[:, t * V :].indirect(far2_sb[:]))
+
+        codes, scales = weave_and_quantize(m0[:], V, "m0")
+        for c, (lo, hi) in enumerate(CHUNKS):
+            product(1, c, codes[:, lo:hi], scales[:, lo:hi])
+
+        m2 = keep.tile([P, PACK, V], F32, name="m2", tag="stage_a", align_bytes=64)
+        for lo, hi in CHUNKS:
+            for t in range(PACK):
+                nc.vector.tensor_copy(m2[:, t, lo:hi], h[:, t * V : (t + 1) * V].indirect(entries(far3_sb, lo, hi)))
+
+        codes, scales = weave_and_quantize(m1[:], V, "m1")
+        for c, (lo, hi) in enumerate(CHUNKS):
+            product(2, c, codes[:, lo:hi], scales[:, lo:hi])
+
+        for c, (lo, hi) in enumerate(CHUNKS):
+            codes, scales = weave_and_quantize(m2[:, :, lo:hi], hi - lo, "m2_%d" % c)
+            product(3, c, codes[:], scales[:])
+            result = keep.tile([P, hi - lo], F32, name="result%d" % c)
+            nc.scalar.activation(result[:], banks[c][:], TANH, bias=bias_sb[:])
+            nc.sync.dma_start(out[:, lo:hi], result[:])

@@ -40,48 +40,49 @@ def tile_picked_yfmm_tanh_p_kernel(
         x_bytes = keep.tile([P, T], U8, name="x_bytes", align_bytes=64)
         nc.vector.memset(x_bytes[:].bitcast(I32), 0)
         offs_sb = load_list(offs, "offs_sb")
-        far1_sb = load_list(far1, "far1_sb")
         close_sb = load_list(close, "close_sb")
         for q in range(4):
             nc.sync.dma_start(
                 x_bytes[32 * q : 32 * q + 4, :].bitcast(I32), x_scales[0, 4 * q : 4 * q + 4, :].bitcast(I32)
             )
-        x_table = keep.tile([P, T], I32, name="x_table", align_bytes=64)
-        nc.sync.dma_start(x_table[:], x_words[0].rearrange("p c r -> p (c r)").bitcast(I32))
-
         w1_rows = w1.rearrange("(p j) c -> p j c", j=PACK)
         w1_raw = []
         for half in range(2):
-            raw = keep.tile([P, PACK, H // 2], F32, name="w1_raw%d" % half, tag="w1_raw%d" % half, align_bytes=64)
+            raw = keep.tile([P, PACK, H // 2], F32, name="w1_raw%d" % half)
             nc.sync.dma_start(raw[:], w1_rows[:, :, half * (H // 2) : (half + 1) * (H // 2)])
             w1_raw.append(raw)
+        x_table = keep.tile([P, T], I32, name="x_table", align_bytes=64)
+        nc.sync.dma_start(x_table[:], x_words[0].rearrange("p c r -> p (c r)").bitcast(I32))
 
         small_raw = []
         for i, mat in enumerate((w2, t1, t2, t3)):
             raw = keep.tile([P, PACK, N], F32, name="small_raw%d" % i)
             nc.sync.dma_start(raw[:], mat.rearrange("(p j) n -> p j n", j=PACK))
             small_raw.append(raw)
+        far1_sb = load_list(far1, "far1_sb")
         far2_sb = load_list(far2, "far2_sb")
         far3_sb = load_list(far3, "far3_sb")
         bias_sb = keep.tile([P, 1], F32, name="bias_sb")
         nc.sync.dma_start(bias_sb[:], bias)
 
         h = keep.tile([P, PACK * V + SPARE], F32, name="h", align_bytes=64)
-        nc.gpsimd.memset(h[:, PACK * V :], 0.0)
+        nc.vector.memset(h[:, PACK * V :], 0.0)
+
+        def plane(t, lo, hi):
+            base = (PACK - 1 - t) * V
+            return h[:, base + lo : base + hi]
 
         warm = keep.tile([P, 1], F32, name="warm")
         nc.scalar.activation(warm[:], h[:, PACK * V : PACK * V + 1], TANH)
 
         pick_bytes = keep.tile([P, S], U8, name="pick_bytes", align_bytes=64)
         nc.vector.tensor_copy(pick_bytes[:], x_bytes[:].indirect(offs_sb[:]))
-        pair_bytes = keep.tile([P, D, V], U8, name="pair_bytes", align_bytes=64)
+        close_bytes = keep.tile([P, V], U8, name="close_bytes", align_bytes=64)
+        nc.vector.tensor_copy(close_bytes[:], x_bytes[:].indirect(close_sb[:]))
+        pair_bytes = keep.tile([P, D, V], U8, name="pair_bytes", tag="stage_b", align_bytes=64)
         nc.vector.tensor_copy(pair_bytes[:], pick_bytes[:].rearrange("p (v d) -> p d v", d=D))
-        pair_words = keep.tile([P, D, V], U32, name="pair_words", align_bytes=64)
-        nc.vector.tensor_copy(
-            pair_words[:].rearrange("p d v -> p v d"), x_table[:].bitcast(U32).indirect(offs_sb[:])
-        )
 
-        w1_bf = [keep.tile([P, 2, P, PACK], BF16, name="w1_bf%d" % u, tag="w1_bf%d" % u, align_bytes=64) for u in range(2)]
+        w1_bf = [keep.tile([P, 2, P, PACK], BF16, name="w1_bf%d" % u, align_bytes=64) for u in range(2)]
         for half in range(2):
             ms = slice(half * (P // 2), (half + 1) * (P // 2))
             src = w1_raw[half][:].rearrange("p j (m t) -> p m j t", t=PACK)
@@ -98,27 +99,42 @@ def tile_picked_yfmm_tanh_p_kernel(
             w1_codes.append(codes)
             w1_scales.append(scales)
 
-        for t in range(PACK):
-            bank = psum.tile([P, V], F32, name="h_bank%d" % t)
+        pair_words = keep.tile([P, D, V], U32, name="pair_words", tag="pair_words", align_bytes=64)
+        for lo, hi in CHUNKS:
+            nc.vector.tensor_copy(
+                pair_words[:, :, lo:hi].rearrange("p d v -> p v d"),
+                x_table[:].bitcast(U32).indirect(entries(offs_sb, D * lo, D * hi)),
+            )
+        close_words = keep.tile([P, V], U32, name="close_words", align_bytes=64)
+        nc.vector.tensor_copy(close_words[:], x_table[:].bitcast(U32).indirect(close_sb[:]))
+
+        def moments(t, bank, lo, hi):
             cols = slice((t % 2) * P, (t % 2 + 1) * P)
             for d in range(D):
                 nc.tensor.matmul_mx(
-                    out=bank[:],
+                    out=bank,
                     lhsT=w1_codes[t // 2][:, cols].bitcast(FP8X4),
                     lhsT_scale=w1_scales[t // 2][:, cols],
-                    rhs=pair_words[:, d, :].bitcast(FP8X4),
-                    rhs_scale=pair_bytes[:, d, :],
+                    rhs=pair_words[:, d, lo:hi].bitcast(FP8X4),
+                    rhs_scale=pair_bytes[:, d, lo:hi],
                     start=(d == 0),
                     stop=(d == D - 1),
                 )
-            nc.scalar.copy(h[:, t * V : (t + 1) * V], bank[:])
 
-        close_bytes = keep.tile([P, V], U8, name="close_bytes", tag="w1_raw1", align_bytes=64)
-        nc.vector.tensor_copy(close_bytes[:], x_bytes[:].indirect(close_sb[:]))
-        close_words = keep.tile([P, V], U32, name="close_words", tag="w1_bf1", align_bytes=64)
-        nc.vector.tensor_copy(close_words[:], x_table[:].bitcast(U32).indirect(close_sb[:]))
+        cut = CHUNKS[-1][0]
+        front = psum.tile([P, cut], F32, name="h_front")
+        for lo, hi in CHUNKS[:-1]:
+            moments(0, front[:, lo:hi], lo, hi)
+        nc.scalar.copy(plane(0, 0, cut), front[:])
+        back = psum.tile([P, V - cut], F32, name="h_back")
+        moments(0, back[:], cut, V)
+        nc.scalar.copy(plane(0, cut, V), back[:])
+        for t in range(1, PACK):
+            bank = psum.tile([P, V], F32, name="h_bank%d" % t)
+            moments(t, bank[:], 0, V)
+            nc.scalar.copy(plane(t, 0, V), bank[:])
 
-        small_bf = keep.tile([P, 4, N, PACK], BF16, name="small_bf", align_bytes=64)
+        small_bf = keep.tile([P, 4, N, PACK], BF16, name="small_bf", tag="pair_words", align_bytes=64)
         for i in range(4):
             nc.scalar.copy(
                 small_bf[:, i].rearrange("p (c e) j -> p c j e", e=4),
@@ -160,29 +176,46 @@ def tile_picked_yfmm_tanh_p_kernel(
 
         m0 = keep.tile([P, PACK, V], F32, name="m0", tag="stage_a", align_bytes=64)
         for t in range(PACK):
-            for lo in (0, V // 2):
-                nc.vector.tensor_copy(
-                    m0[:, t, lo : lo + V // 2], h[:, t * V : (t + 1) * V].indirect(entries(far1_sb, lo, lo + V // 2))
-                )
-        m1 = keep.tile([P, PACK, V], F32, name="m1", align_bytes=64)
+            nc.vector.tensor_copy(m0[:, t, :], plane(t, 0, V + SPARE).indirect(far1_sb[:]))
+        m1 = keep.tile([P, PACK, V], F32, name="m1", tag="stage_b", align_bytes=64)
         for t in range(PACK):
-            nc.vector.tensor_copy(m1[:, t, :], h[:, t * V :].indirect(far2_sb[:]))
+            nc.vector.tensor_copy(m1[:, t, :], plane(t, 0, V + SPARE).indirect(far2_sb[:]))
 
         codes, scales = weave_and_quantize(m0[:], V, "m0")
         for c, (lo, hi) in enumerate(CHUNKS):
             product(1, c, codes[:, lo:hi], scales[:, lo:hi])
 
-        m2 = keep.tile([P, PACK, V], F32, name="m2", tag="stage_a", align_bytes=64)
-        for lo, hi in CHUNKS:
+        def fetch_far3(dst, base, lo, hi):
             for t in range(PACK):
-                nc.vector.tensor_copy(m2[:, t, lo:hi], h[:, t * V : (t + 1) * V].indirect(entries(far3_sb, lo, hi)))
+                nc.vector.tensor_copy(
+                    dst[:, t, lo - base : hi - base], plane(t, 0, V).indirect(entries(far3_sb, lo, hi))
+                )
 
-        codes, scales = weave_and_quantize(m1[:], V, "m1")
-        for c, (lo, hi) in enumerate(CHUNKS):
-            product(2, c, codes[:, lo:hi], scales[:, lo:hi])
+        m2_front = keep.tile([P, PACK, cut], F32, name="m2_front", tag="stage_a", align_bytes=64)
+        for lo, hi in CHUNKS[:-1]:
+            fetch_far3(m2_front, 0, lo, hi)
+
+        half = V // 2
+        codes, scales = weave_and_quantize(m1[:, :, :half], half, "m1_0")
+        product(2, 0, codes[:], scales[:])
+        woven_b = keep.tile([P, half, PACK], BF16, name="m1_1_bf", align_bytes=64)
+        nc.scalar.copy(
+            woven_b[:].rearrange("p (c e) t -> p c t e", e=4), m1[:, :, half:].rearrange("p t (c e) -> p c t e", e=4)
+        )
+        m2_back = keep.tile([P, PACK, V - cut], F32, name="m2_back", tag="stage_b", align_bytes=64)
+        fetch_far3(m2_back, cut, cut, V)
+        codes = keep.tile([P, half], U32, name="m1_1_codes", align_bytes=64)
+        scales = keep.tile([P, half], U8, name="m1_1_scales", align_bytes=64)
+        nc.vector.quantize_mx(
+            out=codes[:].bitcast(FP8X4), scales=scales[:], in_=woven_b[:].rearrange("p c t -> p (c t)")
+        )
+        for c in (1, 2):
+            lo, hi = CHUNKS[c]
+            product(2, c, codes[:, lo - half : hi - half], scales[:, lo - half : hi - half])
 
         for c, (lo, hi) in enumerate(CHUNKS):
-            codes, scales = weave_and_quantize(m2[:, :, lo:hi], hi - lo, "m2_%d" % c)
+            fetched = m2_front[:, :, lo:hi] if hi <= cut else m2_back[:]
+            codes, scales = weave_and_quantize(fetched, hi - lo, "m2_%d" % c)
             product(3, c, codes[:], scales[:])
             result = keep.tile([P, hi - lo], F32, name="result%d" % c)
             nc.scalar.activation(result[:], banks[c][:], TANH, bias=bias_sb[:])

@@ -37,13 +37,20 @@ def tile_picked_yfmm_tanh_p_kernel(
         def entries(tile, lo, hi):
             return tile[:, lo // GROUP : hi // GROUP]
 
+        def quantize(values, name, tag):
+            width = values.shape[1] // PACK
+            codes = keep.tile([P, width], U32, name=name + "_codes", tag=tag, align_bytes=64)
+            scales = keep.tile([P, width], U8, name=name + "_scales", align_bytes=64)
+            nc.vector.quantize_mx(out=codes[:].bitcast(FP8X4), scales=scales[:], in_=values)
+            return codes, scales
+
         x_bytes = keep.tile([P, T], U8, name="x_bytes", align_bytes=64)
         nc.vector.memset(x_bytes[:].bitcast(I32), 0)
         offs_sb = load_list(offs, "offs_sb")
         close_sb = load_list(close, "close_sb")
         for q in range(4):
             nc.sync.dma_start(
-                x_bytes[32 * q : 32 * q + 4, :].bitcast(I32), x_scales[0, 4 * q : 4 * q + 4, :].bitcast(I32)
+                x_bytes[q:P:32, :].bitcast(I32), x_scales[0, q:16:4, :].bitcast(I32)
             )
         w1_rows = w1.rearrange("(p j) c -> p j c", j=PACK)
         w1_raw = []
@@ -88,16 +95,9 @@ def tile_picked_yfmm_tanh_p_kernel(
             src = w1_raw[half][:].rearrange("p j (m t) -> p m j t", t=PACK)
             for u in range(2):
                 nc.scalar.copy(w1_bf[u][:, :, ms, :].rearrange("p t m j -> p m j t"), src[:, :, :, 2 * u : 2 * u + 2])
-        w1_codes = []
-        w1_scales = []
-        for u in range(2):
-            codes = keep.tile([P, 2 * P], U32, name="w1_codes%d" % u, align_bytes=64)
-            scales = keep.tile([P, 2 * P], U8, name="w1_scales%d" % u, align_bytes=64)
-            nc.vector.quantize_mx(
-                out=codes[:].bitcast(FP8X4), scales=scales[:], in_=w1_bf[u][:].rearrange("p t m j -> p (t m j)")
-            )
-            w1_codes.append(codes)
-            w1_scales.append(scales)
+        w1_mx = [
+            quantize(w1_bf[u][:].rearrange("p t m j -> p (t m j)"), "w1_%d" % u, "w1_codes%d" % u) for u in range(2)
+        ]
 
         pair_words = keep.tile([P, D, V], U32, name="pair_words", tag="pair_words", align_bytes=64)
         for lo, hi in CHUNKS:
@@ -113,8 +113,8 @@ def tile_picked_yfmm_tanh_p_kernel(
             for d in range(D):
                 nc.tensor.matmul_mx(
                     out=bank,
-                    lhsT=w1_codes[t // 2][:, cols].bitcast(FP8X4),
-                    lhsT_scale=w1_scales[t // 2][:, cols],
+                    lhsT=w1_mx[t // 2][0][:, cols].bitcast(FP8X4),
+                    lhsT_scale=w1_mx[t // 2][1][:, cols],
                     rhs=pair_words[:, d, lo:hi].bitcast(FP8X4),
                     rhs_scale=pair_bytes[:, d, lo:hi],
                     start=(d == 0),
@@ -134,42 +134,38 @@ def tile_picked_yfmm_tanh_p_kernel(
             moments(t, bank[:], 0, V)
             nc.scalar.copy(plane(t, 0, V), bank[:])
 
-        small_bf = keep.tile([P, 4, N, PACK], BF16, name="small_bf", tag="pair_words", align_bytes=64)
-        for i in range(4):
-            nc.scalar.copy(
-                small_bf[:, i].rearrange("p (c e) j -> p c j e", e=4),
-                small_raw[i][:].rearrange("p j (c e) -> p c j e", e=4),
-            )
-        small_codes = keep.tile([P, 4 * N], U32, name="small_codes", align_bytes=64)
-        small_scales = keep.tile([P, 4 * N], U8, name="small_scales", align_bytes=64)
-        nc.vector.quantize_mx(
-            out=small_codes[:].bitcast(FP8X4), scales=small_scales[:], in_=small_bf[:].rearrange("p i n j -> p (i n j)")
-        )
+        small_bf = []
+        for u, tag in enumerate(("pair_words", "w1_codes1")):
+            rounded = keep.tile([P, 2, N, PACK], BF16, name="small_bf%d" % u, tag=tag, align_bytes=64)
+            for i in range(2):
+                nc.scalar.copy(
+                    rounded[:, i].rearrange("p (c e) j -> p c j e", e=4),
+                    small_raw[2 * u + i][:].rearrange("p j (c e) -> p c j e", e=4),
+                )
+            small_bf.append(rounded[:].rearrange("p i n j -> p (i n j)"))
+        small = [quantize(small_bf[0], "small0", "small0_codes")]
 
         banks = [psum.tile([P, hi - lo], F32, name="out_bank%d" % c) for c, (lo, hi) in enumerate(CHUNKS)]
 
         def product(i, c, codes, scales):
+            cols = slice((i % 2) * N, (i % 2 + 1) * N)
             nc.tensor.matmul_mx(
                 out=banks[c][:],
-                lhsT=small_codes[:, i * N : (i + 1) * N].bitcast(FP8X4),
-                lhsT_scale=small_scales[:, i * N : (i + 1) * N],
+                lhsT=small[i // 2][0][:, cols].bitcast(FP8X4),
+                lhsT_scale=small[i // 2][1][:, cols],
                 rhs=codes.bitcast(FP8X4),
                 rhs_scale=scales,
                 start=(i == 0),
                 stop=(i == 3),
             )
 
-        def weave_and_quantize(fetched, width, name):
-            woven = keep.tile([P, width, PACK], BF16, name=name + "_bf", align_bytes=64)
+        def weave(fetched, name):
+            width = fetched.shape[2]
+            woven = keep.tile([P, width, PACK], BF16, name=name, tag=name, align_bytes=64)
             nc.scalar.copy(
                 woven[:].rearrange("p (c e) t -> p c t e", e=4), fetched.rearrange("p t (c e) -> p c t e", e=4)
             )
-            codes = keep.tile([P, width], U32, name=name + "_codes", align_bytes=64)
-            scales = keep.tile([P, width], U8, name=name + "_scales", align_bytes=64)
-            nc.vector.quantize_mx(
-                out=codes[:].bitcast(FP8X4), scales=scales[:], in_=woven[:].rearrange("p c t -> p (c t)")
-            )
-            return codes, scales
+            return woven[:].rearrange("p c t -> p (c t)")
 
         for c, (lo, hi) in enumerate(CHUNKS):
             product(0, c, close_words[:, lo:hi], close_bytes[:, lo:hi])
@@ -181,42 +177,41 @@ def tile_picked_yfmm_tanh_p_kernel(
         for t in range(PACK):
             nc.vector.tensor_copy(m1[:, t, :], plane(t, 0, V + SPARE).indirect(far2_sb[:]))
 
-        codes, scales = weave_and_quantize(m0[:], V, "m0")
+        codes, scales = quantize(weave(m0[:], "m0_woven"), "m0", "m0_codes")
         for c, (lo, hi) in enumerate(CHUNKS):
             product(1, c, codes[:, lo:hi], scales[:, lo:hi])
 
-        def fetch_far3(dst, base, lo, hi):
+        half = V // 2
+        m2 = []
+        for u, tag in enumerate(("stage_a", "m0_woven")):
+            fetched = keep.tile([P, PACK, half], F32, name="m2_%d" % u, tag=tag, align_bytes=64)
             for t in range(PACK):
                 nc.vector.tensor_copy(
-                    dst[:, t, lo - base : hi - base], plane(t, 0, V).indirect(entries(far3_sb, lo, hi))
+                    fetched[:, t, :], plane(t, 0, V).indirect(entries(far3_sb, u * half, (u + 1) * half))
                 )
+            m2.append(fetched)
+        small.append(quantize(small_bf[1], "small1", "m0_codes"))
 
-        m2_front = keep.tile([P, PACK, cut], F32, name="m2_front", tag="stage_a", align_bytes=64)
-        for lo, hi in CHUNKS[:-1]:
-            fetch_far3(m2_front, 0, lo, hi)
+        m1_woven = [weave(m1[:, :, u * half : (u + 1) * half], "m1_woven%d" % u) for u in range(2)]
+        m2_woven = [
+            weave(m2[lo // half][:, :, lo % half : lo % half + hi - lo], "m2_woven%d" % c)
+            for c, (lo, hi) in enumerate(CHUNKS)
+        ]
 
-        half = V // 2
-        codes, scales = weave_and_quantize(m1[:, :, :half], half, "m1_0")
-        product(2, 0, codes[:], scales[:])
-        woven_b = keep.tile([P, half, PACK], BF16, name="m1_1_bf", align_bytes=64)
-        nc.scalar.copy(
-            woven_b[:].rearrange("p (c e) t -> p c t e", e=4), m1[:, :, half:].rearrange("p t (c e) -> p c t e", e=4)
-        )
-        m2_back = keep.tile([P, PACK, V - cut], F32, name="m2_back", tag="stage_b", align_bytes=64)
-        fetch_far3(m2_back, cut, cut, V)
-        codes = keep.tile([P, half], U32, name="m1_1_codes", align_bytes=64)
-        scales = keep.tile([P, half], U8, name="m1_1_scales", align_bytes=64)
-        nc.vector.quantize_mx(
-            out=codes[:].bitcast(FP8X4), scales=scales[:], in_=woven_b[:].rearrange("p c t -> p (c t)")
-        )
-        for c in (1, 2):
+        def finish(c):
             lo, hi = CHUNKS[c]
-            product(2, c, codes[:, lo - half : hi - half], scales[:, lo - half : hi - half])
-
-        for c, (lo, hi) in enumerate(CHUNKS):
-            fetched = m2_front[:, :, lo:hi] if hi <= cut else m2_back[:]
-            codes, scales = weave_and_quantize(fetched, hi - lo, "m2_%d" % c)
+            codes, scales = quantize(m2_woven[c], "m2q%d" % c, "m2_codes%d" % c)
             product(3, c, codes[:], scales[:])
             result = keep.tile([P, hi - lo], F32, name="result%d" % c)
             nc.scalar.activation(result[:], banks[c][:], TANH, bias=bias_sb[:])
             nc.sync.dma_start(out[:, lo:hi], result[:])
+
+        codes, scales = quantize(m1_woven[0], "m1q0", "m1_codes0")
+        product(2, 0, codes[:], scales[:])
+        finish(0)
+        codes, scales = quantize(m1_woven[1], "m1q1", "stage_a")
+        for c in (1, 2):
+            lo, hi = CHUNKS[c]
+            product(2, c, codes[:, lo - half : hi - half], scales[:, lo - half : hi - half])
+        for c in (1, 2):
+            finish(c)

@@ -18,7 +18,8 @@ P = 128
 PACK = 4
 GROUP = 16
 SPARE = 192
-CHUNKS = ((0, 256), (256, 384), (384, 512))
+CHUNKS = ((0, 128), (128, 256), (256, 384), (384, 512))
+HALVES = ((0, 256), (256, 512))
 
 
 def tile_picked_yfmm_tanh_p_kernel(
@@ -79,9 +80,6 @@ def tile_picked_yfmm_tanh_p_kernel(
             base = (PACK - 1 - t) * V
             return h[:, base + lo : base + hi]
 
-        warm = keep.tile([P, 1], F32, name="warm")
-        nc.scalar.activation(warm[:], h[:, PACK * V : PACK * V + 1], TANH)
-
         pick_bytes = keep.tile([P, S], U8, name="pick_bytes", align_bytes=64)
         nc.vector.tensor_copy(pick_bytes[:], x_bytes[:].indirect(offs_sb[:]))
         close_bytes = keep.tile([P, V], U8, name="close_bytes", align_bytes=64)
@@ -96,11 +94,11 @@ def tile_picked_yfmm_tanh_p_kernel(
             for u in range(2):
                 nc.scalar.copy(w1_bf[u][:, :, ms, :].rearrange("p t m j -> p m j t"), src[:, :, :, 2 * u : 2 * u + 2])
         w1_mx = [
-            quantize(w1_bf[u][:].rearrange("p t m j -> p (t m j)"), "w1_%d" % u, "w1_codes%d" % u) for u in range(2)
+            quantize(w1_bf[0][:, t].rearrange("p m j -> p (m j)"), "w1_%d" % t, "w1_codes%d" % t) for t in range(2)
         ]
 
         pair_words = keep.tile([P, D, V], U32, name="pair_words", tag="pair_words", align_bytes=64)
-        for lo, hi in CHUNKS:
+        for lo, hi in (HALVES[0],) + CHUNKS[2:]:
             nc.vector.tensor_copy(
                 pair_words[:, :, lo:hi].rearrange("p d v -> p v d"),
                 x_table[:].bitcast(U32).indirect(entries(offs_sb, D * lo, D * hi)),
@@ -109,33 +107,32 @@ def tile_picked_yfmm_tanh_p_kernel(
         nc.vector.tensor_copy(close_words[:], x_table[:].bitcast(U32).indirect(close_sb[:]))
 
         def moments(t, bank, lo, hi):
-            cols = slice((t % 2) * P, (t % 2 + 1) * P)
             for d in range(D):
                 nc.tensor.matmul_mx(
                     out=bank,
-                    lhsT=w1_mx[t // 2][0][:, cols].bitcast(FP8X4),
-                    lhsT_scale=w1_mx[t // 2][1][:, cols],
+                    lhsT=w1_mx[t][0][:, :].bitcast(FP8X4),
+                    lhsT_scale=w1_mx[t][1][:, :],
                     rhs=pair_words[:, d, lo:hi].bitcast(FP8X4),
                     rhs_scale=pair_bytes[:, d, lo:hi],
                     start=(d == 0),
                     stop=(d == D - 1),
                 )
 
-        cut = CHUNKS[-1][0]
-        front = psum.tile([P, cut], F32, name="h_front")
-        for lo, hi in CHUNKS[:-1]:
-            moments(0, front[:, lo:hi], lo, hi)
-        nc.scalar.copy(plane(0, 0, cut), front[:])
-        back = psum.tile([P, V - cut], F32, name="h_back")
-        moments(0, back[:], cut, V)
-        nc.scalar.copy(plane(0, cut, V), back[:])
-        for t in range(1, PACK):
+        pieces = [(0, HALVES[0]), (1, HALVES[0]), (0, CHUNKS[2]), (0, CHUNKS[3]), (1, HALVES[1])]
+        for i, (t, (lo, hi)) in enumerate(pieces):
+            bank = psum.tile([P, hi - lo], F32, name="h_piece", tag="bank%d" % i)
+            moments(t, bank[:], lo, hi)
+            nc.scalar.copy(plane(t, lo, hi), bank[:])
+        codes, scales = quantize(w1_bf[1][:].rearrange("p t m j -> p (t m j)"), "w1_23", "w1_codes0")
+        for t in range(2):
+            w1_mx.append((codes[:, t * P : (t + 1) * P], scales[:, t * P : (t + 1) * P]))
+        for t in range(2, PACK):
             bank = psum.tile([P, V], F32, name="h_bank%d" % t)
             moments(t, bank[:], 0, V)
             nc.scalar.copy(plane(t, 0, V), bank[:])
 
         small_bf = []
-        for u, tag in enumerate(("pair_words", "w1_codes1")):
+        for u, tag in enumerate(("pair_words", "w1_codes0")):
             rounded = keep.tile([P, 2, N, PACK], BF16, name="small_bf%d" % u, tag=tag, align_bytes=64)
             for i in range(2):
                 nc.scalar.copy(
@@ -145,7 +142,7 @@ def tile_picked_yfmm_tanh_p_kernel(
             small_bf.append(rounded[:].rearrange("p i n j -> p (i n j)"))
         small = [quantize(small_bf[0], "small0", "small0_codes")]
 
-        banks = [psum.tile([P, hi - lo], F32, name="out_bank%d" % c) for c, (lo, hi) in enumerate(CHUNKS)]
+        banks = [psum.tile([P, hi - lo], F32, name="out_bank%d" % c, tag="bank%d" % c) for c, (lo, hi) in enumerate(CHUNKS)]
 
         def product(i, c, codes, scales):
             cols = slice((i % 2) * N, (i % 2 + 1) * N)
@@ -182,36 +179,26 @@ def tile_picked_yfmm_tanh_p_kernel(
             product(1, c, codes[:, lo:hi], scales[:, lo:hi])
 
         half = V // 2
-        m2 = []
-        for u, tag in enumerate(("stage_a", "m0_woven")):
-            fetched = keep.tile([P, PACK, half], F32, name="m2_%d" % u, tag=tag, align_bytes=64)
-            for t in range(PACK):
-                nc.vector.tensor_copy(
-                    fetched[:, t, :], plane(t, 0, V).indirect(entries(far3_sb, u * half, (u + 1) * half))
-                )
-            m2.append(fetched)
+        m2 = keep.tile([P, PACK, V], F32, name="m2", tag="stage_a", align_bytes=64)
+        for t in range(2):
+            nc.vector.tensor_copy(m2[:, t, :], plane(t, 0, V + SPARE).indirect(far3_sb[:]))
+        for lo, hi in HALVES:
+            for t in range(2, PACK):
+                nc.vector.tensor_copy(m2[:, t, lo:hi], plane(t, 0, V).indirect(entries(far3_sb, lo, hi)))
         small.append(quantize(small_bf[1], "small1", "m0_codes"))
 
-        m1_woven = [weave(m1[:, :, u * half : (u + 1) * half], "m1_woven%d" % u) for u in range(2)]
-        m2_woven = [
-            weave(m2[lo // half][:, :, lo % half : lo % half + hi - lo], "m2_woven%d" % c)
-            for c, (lo, hi) in enumerate(CHUNKS)
-        ]
+        m1_woven = [weave(m1[:, :, lo:hi], "m1_woven%d" % u) for u, (lo, hi) in enumerate(HALVES)]
+        m2_woven = [weave(m2[:, :, lo:hi], "m2_woven%d" % c) for c, (lo, hi) in enumerate(CHUNKS)]
 
-        def finish(c):
-            lo, hi = CHUNKS[c]
+        for u in range(2):
+            codes, scales = quantize(m1_woven[u], "m1q%d" % u, "m1_codes%d" % u)
+            for c in (2 * u, 2 * u + 1):
+                lo, hi = CHUNKS[c]
+                product(2, c, codes[:, lo % half : lo % half + hi - lo], scales[:, lo % half : lo % half + hi - lo])
+        for c, (lo, hi) in enumerate(CHUNKS):
             codes, scales = quantize(m2_woven[c], "m2q%d" % c, "m2_codes%d" % c)
             product(3, c, codes[:], scales[:])
             result = keep.tile([P, hi - lo], F32, name="result%d" % c)
             nc.scalar.activation(result[:], banks[c][:], TANH, bias=bias_sb[:])
-            nc.sync.dma_start(out[:, lo:hi], result[:])
-
-        codes, scales = quantize(m1_woven[0], "m1q0", "m1_codes0")
-        product(2, 0, codes[:], scales[:])
-        finish(0)
-        codes, scales = quantize(m1_woven[1], "m1q1", "stage_a")
-        for c in (1, 2):
-            lo, hi = CHUNKS[c]
-            product(2, c, codes[:, lo - half : hi - half], scales[:, lo - half : hi - half])
-        for c in (1, 2):
-            finish(c)
+            queue = nc.scalar if hi == V else nc.sync
+            queue.dma_start(out[:, lo:hi], result[:])

@@ -28,6 +28,7 @@ def tile_picked_yfmm_tanh_p_kernel(
     nc = tc.nc
     with ExitStack() as ctx:
         keep = ctx.enter_context(tc.tile_pool(name="keep", bufs=1))
+        late = ctx.enter_context(tc.tile_pool(name="late", bufs=1))
         psum = ctx.enter_context(tc.psum_pool(name="psum", bufs=1))
 
         def load_list(src, name):
@@ -53,14 +54,15 @@ def tile_picked_yfmm_tanh_p_kernel(
             nc.sync.dma_start(
                 x_bytes[q:P:32, :].bitcast(I32), x_scales[0, q:16:4, :].bitcast(I32)
             )
-        w1_rows = w1.rearrange("(p j) c -> p j c", j=PACK)
-        w1_raw = []
-        for half in range(2):
-            raw = keep.tile([P, PACK, H // 2], F32, name="w1_raw%d" % half)
-            nc.sync.dma_start(raw[:], w1_rows[:, :, half * (H // 2) : (half + 1) * (H // 2)])
-            w1_raw.append(raw)
         x_table = keep.tile([P, T], I32, name="x_table", align_bytes=64)
         nc.sync.dma_start(x_table[:], x_words[0].rearrange("p c r -> p (c r)").bitcast(I32))
+        w1_rows = w1.rearrange("(p j) c -> p j c", j=PACK)
+        w1_raw = [
+            keep.tile([P, PACK, H // 2], F32, name="w1_raw0"),
+            late.tile([P, PACK, H // 2], F32, name="w1_raw1", offset=0, align_bytes=64),
+        ]
+        for half in range(2):
+            nc.sync.dma_start(w1_raw[half][:], w1_rows[:, :, half * (H // 2) : (half + 1) * (H // 2)])
 
         small_raw = []
         for i, mat in enumerate((w2, t1, t2, t3)):
@@ -82,10 +84,12 @@ def tile_picked_yfmm_tanh_p_kernel(
 
         pick_bytes = keep.tile([P, S], U8, name="pick_bytes", align_bytes=64)
         nc.vector.tensor_copy(pick_bytes[:], x_bytes[:].indirect(offs_sb[:]))
-        close_bytes = keep.tile([P, V], U8, name="close_bytes", align_bytes=64)
-        nc.vector.tensor_copy(close_bytes[:], x_bytes[:].indirect(close_sb[:]))
+        pair_words = keep.tile([P, D, V], U32, name="pair_words", tag="pair_words", align_bytes=64)
+        nc.vector.tensor_copy(pair_words[:].rearrange("p d v -> p v d"), x_table[:].bitcast(U32).indirect(offs_sb[:]))
         pair_bytes = keep.tile([P, D, V], U8, name="pair_bytes", tag="stage_b", align_bytes=64)
         nc.vector.tensor_copy(pair_bytes[:], pick_bytes[:].rearrange("p (v d) -> p d v", d=D))
+        close_bytes = [keep.tile([P, V // 2], U8, name="close_bytes0", align_bytes=64)]
+        nc.vector.tensor_copy(close_bytes[0][:], x_bytes[:].indirect(entries(close_sb, *HALVES[0])))
 
         w1_bf = [keep.tile([P, 2, P, PACK], BF16, name="w1_bf%d" % u, align_bytes=64) for u in range(2)]
         for half in range(2):
@@ -93,17 +97,15 @@ def tile_picked_yfmm_tanh_p_kernel(
             src = w1_raw[half][:].rearrange("p j (m t) -> p m j t", t=PACK)
             for u in range(2):
                 nc.scalar.copy(w1_bf[u][:, :, ms, :].rearrange("p t m j -> p m j t"), src[:, :, :, 2 * u : 2 * u + 2])
-        w1_mx = [
-            quantize(w1_bf[0][:, t].rearrange("p m j -> p (m j)"), "w1_%d" % t, "w1_codes%d" % t) for t in range(2)
-        ]
+        w1_mx = []
+        for u in range(2):
+            codes, scales = quantize(w1_bf[u][:].rearrange("p t m j -> p (t m j)"), "w1_%d" % u, "w1_codes%d" % u)
+            for t in range(2):
+                w1_mx.append((codes[:, t * P : (t + 1) * P], scales[:, t * P : (t + 1) * P]))
 
-        pair_words = keep.tile([P, D, V], U32, name="pair_words", tag="pair_words", align_bytes=64)
-        for lo, hi in (HALVES[0],) + CHUNKS[2:]:
-            nc.vector.tensor_copy(
-                pair_words[:, :, lo:hi].rearrange("p d v -> p v d"),
-                x_table[:].bitcast(U32).indirect(entries(offs_sb, D * lo, D * hi)),
-            )
-        close_words = keep.tile([P, V], U32, name="close_words", align_bytes=64)
+        close_bytes.append(late.tile([P, V // 2], U8, name="close_bytes1", offset=4 * V, align_bytes=64))
+        nc.vector.tensor_copy(close_bytes[1][:], x_bytes[:].indirect(entries(close_sb, *HALVES[1])))
+        close_words = late.tile([P, V], U32, name="close_words", offset=0, align_bytes=64)
         nc.vector.tensor_copy(close_words[:], x_table[:].bitcast(U32).indirect(close_sb[:]))
 
         def moments(t, bank, lo, hi):
@@ -118,21 +120,18 @@ def tile_picked_yfmm_tanh_p_kernel(
                     stop=(d == D - 1),
                 )
 
-        pieces = [(0, HALVES[0]), (1, HALVES[0]), (0, CHUNKS[2]), (0, CHUNKS[3]), (1, HALVES[1])]
-        for i, (t, (lo, hi)) in enumerate(pieces):
-            bank = psum.tile([P, hi - lo], F32, name="h_piece", tag="bank%d" % i)
-            moments(t, bank[:], lo, hi)
-            nc.scalar.copy(plane(t, lo, hi), bank[:])
-        codes, scales = quantize(w1_bf[1][:].rearrange("p t m j -> p (t m j)"), "w1_23", "w1_codes0")
         for t in range(2):
-            w1_mx.append((codes[:, t * P : (t + 1) * P], scales[:, t * P : (t + 1) * P]))
+            for u, (lo, hi) in enumerate(HALVES):
+                bank = psum.tile([P, hi - lo], F32, name="h_half", tag="bank%d" % (2 * t + u))
+                moments(t, bank[:], lo, hi)
+                nc.scalar.copy(plane(t, lo, hi), bank[:])
         for t in range(2, PACK):
             bank = psum.tile([P, V], F32, name="h_bank%d" % t)
             moments(t, bank[:], 0, V)
             nc.scalar.copy(plane(t, 0, V), bank[:])
 
         small_bf = []
-        for u, tag in enumerate(("pair_words", "w1_codes0")):
+        for u, tag in enumerate(("pair_words", "w1_codes1")):
             rounded = keep.tile([P, 2, N, PACK], BF16, name="small_bf%d" % u, tag=tag, align_bytes=64)
             for i in range(2):
                 nc.scalar.copy(
@@ -165,7 +164,7 @@ def tile_picked_yfmm_tanh_p_kernel(
             return woven[:].rearrange("p c t -> p (c t)")
 
         for c, (lo, hi) in enumerate(CHUNKS):
-            product(0, c, close_words[:, lo:hi], close_bytes[:, lo:hi])
+            product(0, c, close_words[:, lo:hi], close_bytes[c // 2][:, lo % (V // 2) : lo % (V // 2) + hi - lo])
 
         m0 = keep.tile([P, PACK, V], F32, name="m0", tag="stage_a", align_bytes=64)
         for t in range(PACK):

@@ -166,38 +166,44 @@ def tile_picked_yfmm_tanh_p_kernel(
         for c, (lo, hi) in enumerate(CHUNKS):
             product(0, c, close_words[:, lo:hi], close_bytes[c // 2][:, lo % (V // 2) : lo % (V // 2) + hi - lo])
 
-        m0 = keep.tile([P, PACK, V], F32, name="m0", tag="stage_a", align_bytes=64)
+        m0 = late.tile([P, PACK + 1, V], F32, name="m0", offset=8 * V, align_bytes=64)
         for t in range(PACK):
             nc.vector.tensor_copy(m0[:, t, :], plane(t, 0, V + SPARE).indirect(far1_sb[:]))
         m1 = keep.tile([P, PACK, V], F32, name="m1", tag="stage_b", align_bytes=64)
         for t in range(PACK):
             nc.vector.tensor_copy(m1[:, t, :], plane(t, 0, V + SPARE).indirect(far2_sb[:]))
 
-        codes, scales = quantize(weave(m0[:], "m0_woven"), "m0", "m0_codes")
-        for c, (lo, hi) in enumerate(CHUNKS):
-            product(1, c, codes[:, lo:hi], scales[:, lo:hi])
-
         half = V // 2
-        m2 = keep.tile([P, PACK, V], F32, name="m2", tag="stage_a", align_bytes=64)
+
+        def far_half(i, u, woven):
+            codes, scales = quantize(woven, "m%dq%d" % (i, u), "m%d_codes%d" % (i, u))
+            for c in (2 * u, 2 * u + 1):
+                lo, hi = CHUNKS[c]
+                product(i + 1, c, codes[:, lo % half : lo % half + hi - lo], scales[:, lo % half : lo % half + hi - lo])
+
+        m0_woven = [weave(m0[:, :PACK, lo:hi], "m0_woven%d" % u) for u, (lo, hi) in enumerate(HALVES)]
+        far_half(0, 0, m0_woven[0])
+
+        m2 = late.tile([P, PACK, V], F32, name="m2", offset=8 * V, align_bytes=64)
         for t in range(2):
             nc.vector.tensor_copy(m2[:, t, :], plane(t, 0, V + SPARE).indirect(far3_sb[:]))
         for lo, hi in HALVES:
             for t in range(2, PACK):
                 nc.vector.tensor_copy(m2[:, t, lo:hi], plane(t, 0, V).indirect(entries(far3_sb, lo, hi)))
-        small.append(quantize(small_bf[1], "small1", "m0_codes"))
+        far_half(0, 1, m0_woven[1])
+        codes = late.tile([P, 2 * N], U32, name="small1_codes", offset=24 * V, align_bytes=64)
+        scales = keep.tile([P, 2 * N], U8, name="small1_scales", align_bytes=64)
+        nc.vector.quantize_mx(out=codes[:].bitcast(FP8X4), scales=scales[:], in_=small_bf[1])
+        small.append((codes, scales))
 
         m1_woven = [weave(m1[:, :, lo:hi], "m1_woven%d" % u) for u, (lo, hi) in enumerate(HALVES)]
         m2_woven = [weave(m2[:, :, lo:hi], "m2_woven%d" % c) for c, (lo, hi) in enumerate(CHUNKS)]
 
         for u in range(2):
-            codes, scales = quantize(m1_woven[u], "m1q%d" % u, "m1_codes%d" % u)
-            for c in (2 * u, 2 * u + 1):
-                lo, hi = CHUNKS[c]
-                product(2, c, codes[:, lo % half : lo % half + hi - lo], scales[:, lo % half : lo % half + hi - lo])
+            far_half(1, u, m1_woven[u])
         for c, (lo, hi) in enumerate(CHUNKS):
             codes, scales = quantize(m2_woven[c], "m2q%d" % c, "m2_codes%d" % c)
             product(3, c, codes[:], scales[:])
             result = keep.tile([P, hi - lo], F32, name="result%d" % c)
             nc.scalar.activation(result[:], banks[c][:], TANH, bias=bias_sb[:])
-            queue = nc.scalar if hi == V else nc.sync
-            queue.dma_start(out[:, lo:hi], result[:])
+            nc.sync.dma_start(out[:, lo:hi], result[:])

@@ -88,8 +88,8 @@ def tile_picked_yfmm_tanh_p_kernel(
         nc.vector.tensor_copy(pair_words[:].rearrange("p d v -> p v d"), x_table[:].bitcast(U32).indirect(offs_sb[:]))
         pair_bytes = keep.tile([P, D, V], U8, name="pair_bytes", tag="stage_b", align_bytes=64)
         nc.vector.tensor_copy(pair_bytes[:], pick_bytes[:].rearrange("p (v d) -> p d v", d=D))
-        close_bytes = [keep.tile([P, V // 2], U8, name="close_bytes0", align_bytes=64)]
-        nc.vector.tensor_copy(close_bytes[0][:], x_bytes[:].indirect(entries(close_sb, *HALVES[0])))
+        close_bytes = keep.tile([P, V], U8, name="close_bytes", align_bytes=64)
+        nc.vector.tensor_copy(close_bytes[:], x_bytes[:].indirect(close_sb[:]))
 
         w1_bf = [keep.tile([P, 2, P, PACK], BF16, name="w1_bf%d" % u, align_bytes=64) for u in range(2)]
         for half in range(2):
@@ -97,14 +97,13 @@ def tile_picked_yfmm_tanh_p_kernel(
             src = w1_raw[half][:].rearrange("p j (m t) -> p m j t", t=PACK)
             for u in range(2):
                 nc.scalar.copy(w1_bf[u][:, :, ms, :].rearrange("p t m j -> p m j t"), src[:, :, :, 2 * u : 2 * u + 2])
-        w1_mx = []
-        for u in range(2):
-            codes, scales = quantize(w1_bf[u][:].rearrange("p t m j -> p (t m j)"), "w1_%d" % u, "w1_codes%d" % u)
-            for t in range(2):
-                w1_mx.append((codes[:, t * P : (t + 1) * P], scales[:, t * P : (t + 1) * P]))
+        w1_mx = [
+            quantize(w1_bf[0][:, t].rearrange("p m j -> p (m j)"), "w1_%d" % t, "w1_plane%d" % t) for t in range(2)
+        ]
+        codes, scales = quantize(w1_bf[1][:].rearrange("p t m j -> p (t m j)"), "w1_23", "w1_codes1")
+        for t in range(2):
+            w1_mx.append((codes[:, t * P : (t + 1) * P], scales[:, t * P : (t + 1) * P]))
 
-        close_bytes.append(late.tile([P, V // 2], U8, name="close_bytes1", offset=4 * V, align_bytes=64))
-        nc.vector.tensor_copy(close_bytes[1][:], x_bytes[:].indirect(entries(close_sb, *HALVES[1])))
         close_words = late.tile([P, V], U32, name="close_words", offset=0, align_bytes=64)
         nc.vector.tensor_copy(close_words[:], x_table[:].bitcast(U32).indirect(close_sb[:]))
 
@@ -120,11 +119,11 @@ def tile_picked_yfmm_tanh_p_kernel(
                     stop=(d == D - 1),
                 )
 
-        for t in range(2):
-            for u, (lo, hi) in enumerate(HALVES):
-                bank = psum.tile([P, hi - lo], F32, name="h_half", tag="bank%d" % (2 * t + u))
-                moments(t, bank[:], lo, hi)
-                nc.scalar.copy(plane(t, lo, hi), bank[:])
+        pieces = [(0, HALVES[0]), (0, CHUNKS[2]), (0, CHUNKS[3]), (1, HALVES[0]), (1, HALVES[1])]
+        for i, (t, (lo, hi)) in enumerate(pieces):
+            bank = psum.tile([P, hi - lo], F32, name="h_piece", tag="bank%d" % i)
+            moments(t, bank[:], lo, hi)
+            nc.scalar.copy(plane(t, lo, hi), bank[:])
         for t in range(2, PACK):
             bank = psum.tile([P, V], F32, name="h_bank%d" % t)
             moments(t, bank[:], 0, V)
@@ -164,7 +163,7 @@ def tile_picked_yfmm_tanh_p_kernel(
             return woven[:].rearrange("p c t -> p (c t)")
 
         for c, (lo, hi) in enumerate(CHUNKS):
-            product(0, c, close_words[:, lo:hi], close_bytes[c // 2][:, lo % (V // 2) : lo % (V // 2) + hi - lo])
+            product(0, c, close_words[:, lo:hi], close_bytes[:, lo:hi])
 
         m0 = late.tile([P, PACK + 1, V], F32, name="m0", offset=8 * V, align_bytes=64)
         for t in range(PACK):

@@ -29,6 +29,7 @@ def tile_picked_yfmm_tanh_p_kernel(
     with ExitStack() as ctx:
         keep = ctx.enter_context(tc.tile_pool(name="keep", bufs=1))
         late = ctx.enter_context(tc.tile_pool(name="late", bufs=1))
+        early = ctx.enter_context(tc.tile_pool(name="early", bufs=1))
         psum = ctx.enter_context(tc.psum_pool(name="psum", bufs=1))
 
         def load_list(src, name):
@@ -50,10 +51,7 @@ def tile_picked_yfmm_tanh_p_kernel(
         nc.vector.memset(x_bytes[:].bitcast(I32), 0)
         offs_sb = load_list(offs, "offs_sb")
         close_sb = load_list(close, "close_sb")
-        for q in range(4):
-            nc.sync.dma_start(
-                x_bytes[q:P:32, :].bitcast(I32), x_scales[0, q:16:4, :].bitcast(I32)
-            )
+        nc.sync.dma_start(x_bytes[0:P:8, :].bitcast(I32), x_scales[0].bitcast(I32))
         x_table = keep.tile([P, T], I32, name="x_table", align_bytes=64)
         nc.sync.dma_start(x_table[:], x_words[0].rearrange("p c r -> p (c r)").bitcast(I32))
         w1_rows = w1.rearrange("(p j) c -> p j c", j=PACK)
@@ -64,16 +62,9 @@ def tile_picked_yfmm_tanh_p_kernel(
         for half in range(2):
             nc.sync.dma_start(w1_raw[half][:], w1_rows[:, :, half * (H // 2) : (half + 1) * (H // 2)])
 
-        small_raw = []
-        for i, mat in enumerate((w2, t1, t2, t3)):
-            raw = keep.tile([P, PACK, N], F32, name="small_raw%d" % i)
-            nc.sync.dma_start(raw[:], mat.rearrange("(p j) n -> p j n", j=PACK))
-            small_raw.append(raw)
         far1_sb = load_list(far1, "far1_sb")
         far2_sb = load_list(far2, "far2_sb")
         far3_sb = load_list(far3, "far3_sb")
-        bias_sb = keep.tile([P, 1], F32, name="bias_sb")
-        nc.sync.dma_start(bias_sb[:], bias)
 
         h = keep.tile([P, PACK * V + SPARE], F32, name="h", align_bytes=64)
         nc.vector.memset(h[:, PACK * V :], 0.0)
@@ -82,14 +73,31 @@ def tile_picked_yfmm_tanh_p_kernel(
             base = (PACK - 1 - t) * V
             return h[:, base + lo : base + hi]
 
-        pick_bytes = keep.tile([P, S], U8, name="pick_bytes", align_bytes=64)
-        nc.vector.tensor_copy(pick_bytes[:], x_bytes[:].indirect(offs_sb[:]))
+        pick_tile = early.tile([P, 17 * V], U8, name="pick_bytes", offset=0, align_bytes=64)
+        pick_bytes = pick_tile[:, :S]
+        nc.vector.tensor_copy(pick_bytes, x_bytes[:].indirect(offs_sb[:]))
         pair_words = keep.tile([P, D, V], U32, name="pair_words", tag="pair_words", align_bytes=64)
         nc.vector.tensor_copy(pair_words[:].rearrange("p d v -> p v d"), x_table[:].bitcast(U32).indirect(offs_sb[:]))
-        pair_bytes = keep.tile([P, D, V], U8, name="pair_bytes", tag="stage_b", align_bytes=64)
-        nc.vector.tensor_copy(pair_bytes[:], pick_bytes[:].rearrange("p (v d) -> p d v", d=D))
-        close_bytes = keep.tile([P, V], U8, name="close_bytes", align_bytes=64)
-        nc.vector.tensor_copy(close_bytes[:], x_bytes[:].indirect(close_sb[:]))
+        parted = keep.tile([P, S], U8, name="parted", align_bytes=64)
+        nc.vector.tensor_copy(parted[:].rearrange("p (d v) -> p d v", d=D), pick_bytes.rearrange("p (v d) -> p d v", d=D))
+        close_picked = keep.tile([P, V], U8, name="close_picked", align_bytes=64)
+        nc.vector.tensor_copy(close_picked[:], x_bytes[:].indirect(close_sb[:]))
+
+        def place_rows(dst, src):
+            for r in range(4):
+                nc.sync.dma_start(dst[r:P:32, :].bitcast(I32), src[8 * r : P : 32, :].bitcast(I32))
+
+        pair_flat = keep.tile([P, S], U8, name="pair_bytes", tag="stage_b", align_bytes=64)
+        place_rows(pair_flat, parted)
+        pair_bytes = pair_flat[:].rearrange("p (d v) -> p d v", d=D)
+
+        small_raw = []
+        for i, mat in enumerate((w2, t1, t2, t3)):
+            raw = early.tile([P, PACK, N], F32, name="small_raw%d" % i, offset=4 * V * i, align_bytes=64)
+            nc.sync.dma_start(raw[:], mat.rearrange("(p j) n -> p j n", j=PACK))
+            small_raw.append(raw)
+        bias_sb = early.tile([P, 1], F32, name="bias_sb", offset=16 * V, align_bytes=64)
+        nc.sync.dma_start(bias_sb[:], bias)
 
         w1_bf = [keep.tile([P, 2, P, PACK], BF16, name="w1_bf%d" % u, align_bytes=64) for u in range(2)]
         for half in range(2):
@@ -104,6 +112,8 @@ def tile_picked_yfmm_tanh_p_kernel(
         for t in range(2):
             w1_mx.append((codes[:, t * P : (t + 1) * P], scales[:, t * P : (t + 1) * P]))
 
+        close_bytes = late.tile([P, V], U8, name="close_bytes", offset=4 * V, align_bytes=64)
+        place_rows(close_bytes, close_picked)
         close_words = late.tile([P, V], U32, name="close_words", offset=0, align_bytes=64)
         nc.vector.tensor_copy(close_words[:], x_table[:].bitcast(U32).indirect(close_sb[:]))
 

@@ -48,10 +48,13 @@ def tile_picked_yfmm_tanh_p_kernel(
             return codes, scales
 
         x_bytes = keep.tile([P, T], U8, name="x_bytes", align_bytes=64)
-        nc.vector.memset(x_bytes[:].bitcast(I32), 0)
+        nc.sync.dma_start(
+            x_bytes[0:32, :].bitcast(I32), x_scales[0].bitcast(I32).unsqueeze(1).to_broadcast([16, 2, T // 4])
+        )
+        nc.vector.memset(x_bytes[32:64, :].bitcast(I32), 0)
+        nc.vector.memset(x_bytes[64:P, :].bitcast(I32), 0)
         offs_sb = load_list(offs, "offs_sb")
         close_sb = load_list(close, "close_sb")
-        nc.sync.dma_start(x_bytes[0:P:8, :].bitcast(I32), x_scales[0].bitcast(I32))
         x_table = keep.tile([P, T], I32, name="x_table", align_bytes=64)
         nc.sync.dma_start(x_table[:], x_words[0].rearrange("p c r -> p (c r)").bitcast(I32))
         w1_rows = w1.rearrange("(p j) c -> p j c", j=PACK)
@@ -83,12 +86,12 @@ def tile_picked_yfmm_tanh_p_kernel(
         close_picked = keep.tile([P, V], U8, name="close_picked", align_bytes=64)
         nc.vector.tensor_copy(close_picked[:], x_bytes[:].indirect(close_sb[:]))
 
-        def place_rows(dst, src):
+        def place_rows(dst, src, first):
             for r in range(4):
-                nc.sync.dma_start(dst[r:P:32, :].bitcast(I32), src[8 * r : P : 32, :].bitcast(I32))
+                nc.sync.dma_start(dst[r:P:32, :].bitcast(I32), src[2 * r + first : 32 : 8, :].bitcast(I32))
 
         pair_flat = keep.tile([P, S], U8, name="pair_bytes", tag="stage_b", align_bytes=64)
-        place_rows(pair_flat, parted)
+        place_rows(pair_flat, parted, 0)
         pair_bytes = pair_flat[:].rearrange("p (d v) -> p d v", d=D)
 
         small_raw = []
@@ -113,7 +116,7 @@ def tile_picked_yfmm_tanh_p_kernel(
             w1_mx.append((codes[:, t * P : (t + 1) * P], scales[:, t * P : (t + 1) * P]))
 
         close_bytes = late.tile([P, V], U8, name="close_bytes", offset=4 * V, align_bytes=64)
-        place_rows(close_bytes, close_picked)
+        place_rows(close_bytes, close_picked, 1)
         close_words = late.tile([P, V], U32, name="close_words", offset=0, align_bytes=64)
         nc.vector.tensor_copy(close_words[:], x_table[:].bitcast(U32).indirect(close_sb[:]))
 
@@ -148,16 +151,16 @@ def tile_picked_yfmm_tanh_p_kernel(
                     small_raw[2 * u + i][:].rearrange("p j (c e) -> p c j e", e=4),
                 )
             small_bf.append(rounded[:].rearrange("p i n j -> p (i n j)"))
-        small = [quantize(small_bf[0], "small0", "small0_codes")]
+        codes, scales = quantize(small_bf[0], "small0", "small0_codes")
+        small = [(codes[:, i * N : (i + 1) * N], scales[:, i * N : (i + 1) * N]) for i in range(2)]
 
         banks = [psum.tile([P, hi - lo], F32, name="out_bank%d" % c, tag="bank%d" % c) for c, (lo, hi) in enumerate(CHUNKS)]
 
         def product(i, c, codes, scales):
-            cols = slice((i % 2) * N, (i % 2 + 1) * N)
             nc.tensor.matmul_mx(
                 out=banks[c][:],
-                lhsT=small[i // 2][0][:, cols].bitcast(FP8X4),
-                lhsT_scale=small[i // 2][1][:, cols],
+                lhsT=small[i][0][:, :].bitcast(FP8X4),
+                lhsT_scale=small[i][1][:, :],
                 rhs=codes.bitcast(FP8X4),
                 rhs_scale=scales,
                 start=(i == 0),
@@ -200,9 +203,9 @@ def tile_picked_yfmm_tanh_p_kernel(
             for t in range(2, PACK):
                 nc.vector.tensor_copy(m2[:, t, lo:hi], plane(t, 0, V).indirect(entries(far3_sb, lo, hi)))
         far_half(0, 1, m0_woven[1])
-        codes = late.tile([P, 2 * N], U32, name="small1_codes", offset=24 * V, align_bytes=64)
-        scales = keep.tile([P, 2 * N], U8, name="small1_scales", align_bytes=64)
-        nc.vector.quantize_mx(out=codes[:].bitcast(FP8X4), scales=scales[:], in_=small_bf[1])
+        codes = late.tile([P, N], U32, name="t2_codes", offset=24 * V, align_bytes=64)
+        scales = keep.tile([P, N], U8, name="t2_scales", align_bytes=64)
+        nc.vector.quantize_mx(out=codes[:].bitcast(FP8X4), scales=scales[:], in_=small_bf[1][:, : PACK * N])
         small.append((codes, scales))
 
         m1_woven = [weave(m1[:, :, lo:hi], "m1_woven%d" % u) for u, (lo, hi) in enumerate(HALVES)]
@@ -210,6 +213,7 @@ def tile_picked_yfmm_tanh_p_kernel(
 
         for u in range(2):
             far_half(1, u, m1_woven[u])
+        small.append(quantize(small_bf[1][:, PACK * N :], "t3", "stage_b"))
         for c, (lo, hi) in enumerate(CHUNKS):
             codes, scales = quantize(m2_woven[c], "m2q%d" % c, "m2_codes%d" % c)
             product(3, c, codes[:], scales[:])

@@ -78,13 +78,18 @@ def tile_picked_yfmm_tanh_p_kernel(
 
         pick_tile = early.tile([P, 17 * V], U8, name="pick_bytes", offset=0, align_bytes=64)
         pick_bytes = pick_tile[:, :S]
-        nc.vector.tensor_copy(pick_bytes, x_bytes[:].indirect(offs_sb[:]))
+        for lo, hi in HALVES:
+            nc.vector.tensor_copy(pick_bytes[:, D * lo : D * hi], x_bytes[:].indirect(entries(offs_sb, D * lo, D * hi)))
+        close_words = keep.tile([P, V], U32, name="close_words", align_bytes=64)
+        nc.vector.tensor_copy(close_words[:], x_table[:].bitcast(U32).indirect(close_sb[:]))
         pair_words = keep.tile([P, D, V], U32, name="pair_words", tag="pair_words", align_bytes=64)
         nc.vector.tensor_copy(pair_words[:].rearrange("p d v -> p v d"), x_table[:].bitcast(U32).indirect(offs_sb[:]))
         parted = keep.tile([P, S], U8, name="parted", align_bytes=64)
-        nc.vector.tensor_copy(parted[:].rearrange("p (d v) -> p d v", d=D), pick_bytes.rearrange("p (v d) -> p d v", d=D))
-        close_picked = keep.tile([P, V], U8, name="close_picked", align_bytes=64)
-        nc.vector.tensor_copy(close_picked[:], x_bytes[:].indirect(close_sb[:]))
+        for lo, hi in HALVES:
+            nc.vector.tensor_copy(
+                parted[:].rearrange("p (d v) -> p d v", d=D)[:, :, lo:hi],
+                pick_bytes[:, D * lo : D * hi].rearrange("p (v d) -> p d v", d=D),
+            )
 
         def place_rows(dst, src, first):
             for r in range(4):
@@ -115,10 +120,22 @@ def tile_picked_yfmm_tanh_p_kernel(
         for t in range(2):
             w1_mx.append((codes[:, t * P : (t + 1) * P], scales[:, t * P : (t + 1) * P]))
 
-        close_bytes = late.tile([P, V], U8, name="close_bytes", offset=4 * V, align_bytes=64)
+        close_picked = late.tile([P, V], U8, name="close_picked", offset=0, align_bytes=64)
+        nc.vector.tensor_copy(close_picked[:], x_bytes[:].indirect(close_sb[:]))
+        close_bytes = keep.tile([P, V], U8, name="close_bytes", align_bytes=64)
         place_rows(close_bytes, close_picked, 1)
-        close_words = late.tile([P, V], U32, name="close_words", offset=0, align_bytes=64)
-        nc.vector.tensor_copy(close_words[:], x_table[:].bitcast(U32).indirect(close_sb[:]))
+
+        warm = psum.tile([P, V], F32, name="warm", tag="h_bank3")
+        for i in range(3):
+            nc.tensor.matmul_mx(
+                out=warm[:],
+                lhsT=close_words[:, :P].bitcast(FP8X4),
+                lhsT_scale=parted[:, :P],
+                rhs=close_words[:].bitcast(FP8X4),
+                rhs_scale=parted[:, :V],
+                start=True,
+                stop=True,
+            )
 
         def moments(t, bank, lo, hi):
             for d in range(D):
@@ -138,7 +155,7 @@ def tile_picked_yfmm_tanh_p_kernel(
             moments(t, bank[:], lo, hi)
             nc.scalar.copy(plane(t, lo, hi), bank[:])
         for t in range(2, PACK):
-            bank = psum.tile([P, V], F32, name="h_bank%d" % t)
+            bank = psum.tile([P, V], F32, name="h_bank%d" % t, tag="h_bank%d" % t)
             moments(t, bank[:], 0, V)
             nc.scalar.copy(plane(t, 0, V), bank[:])
 

@@ -70,33 +70,34 @@ def tile_picked_yfmm_tanh_p_kernel(
         far3_sb = load_list(far3, "far3_sb")
 
         h = keep.tile([P, PACK * V + SPARE], F32, name="h", align_bytes=64)
-        nc.vector.memset(h[:, PACK * V :], 0.0)
+        nc.vector.memset(h[:, PACK * V : PACK * V + SPARE // 2], 0.0)
+        nc.scalar.copy(h[:, PACK * V + SPARE // 2 :], h[:, PACK * V : PACK * V + SPARE // 2])
 
         def plane(t, lo, hi):
             base = (PACK - 1 - t) * V
             return h[:, base + lo : base + hi]
 
-        pick_tile = early.tile([P, 17 * V], U8, name="pick_bytes", offset=0, align_bytes=64)
-        pick_bytes = pick_tile[:, :S]
+        pick_bytes = keep.tile([P, S], U8, name="pick_bytes", align_bytes=64)
         for lo, hi in HALVES:
             nc.vector.tensor_copy(pick_bytes[:, D * lo : D * hi], x_bytes[:].indirect(entries(offs_sb, D * lo, D * hi)))
         close_words = keep.tile([P, V], U32, name="close_words", align_bytes=64)
         nc.vector.tensor_copy(close_words[:], x_table[:].bitcast(U32).indirect(close_sb[:]))
         pair_words = keep.tile([P, D, V], U32, name="pair_words", tag="pair_words", align_bytes=64)
         nc.vector.tensor_copy(pair_words[:].rearrange("p d v -> p v d"), x_table[:].bitcast(U32).indirect(offs_sb[:]))
-        parted = keep.tile([P, S], U8, name="parted", align_bytes=64)
+        parted_tile = early.tile([P, 17 * V], U8, name="parted", offset=0, align_bytes=64)
+        parted = parted_tile[:, :S]
         for lo, hi in HALVES:
             nc.vector.tensor_copy(
-                parted[:].rearrange("p (d v) -> p d v", d=D)[:, :, lo:hi],
+                parted.rearrange("p (d v) -> p d v", d=D)[:, :, lo:hi],
                 pick_bytes[:, D * lo : D * hi].rearrange("p (v d) -> p d v", d=D),
             )
 
-        def place_rows(dst, src, first):
+        def place_rows(dst, src, first, queue):
             for r in range(4):
-                nc.sync.dma_start(dst[r:P:32, :].bitcast(I32), src[2 * r + first : 32 : 8, :].bitcast(I32))
+                queue.dma_start(dst[r:P:32, :].bitcast(I32), src[2 * r + first : 32 : 8, :].bitcast(I32))
 
         pair_flat = keep.tile([P, S], U8, name="pair_bytes", tag="stage_b", align_bytes=64)
-        place_rows(pair_flat, parted, 0)
+        place_rows(pair_flat, parted, 0, nc.scalar)
         pair_bytes = pair_flat[:].rearrange("p (d v) -> p d v", d=D)
 
         small_raw = []
@@ -123,7 +124,7 @@ def tile_picked_yfmm_tanh_p_kernel(
         close_picked = late.tile([P, V], U8, name="close_picked", offset=0, align_bytes=64)
         nc.vector.tensor_copy(close_picked[:], x_bytes[:].indirect(close_sb[:]))
         close_bytes = keep.tile([P, V], U8, name="close_bytes", align_bytes=64)
-        place_rows(close_bytes, close_picked, 1)
+        place_rows(close_bytes, close_picked, 1, nc.sync)
 
         warm = psum.tile([P, V], F32, name="warm", tag="h_bank3")
         for i in range(3):

@@ -13,6 +13,7 @@ U16 = mybir.dt.uint16
 U8 = mybir.dt.uint8
 FP8X4 = mybir.dt.float8_e4m3fn_x4
 TANH = mybir.ActivationFunctionType.Tanh
+COPY = mybir.ActivationFunctionType.Copy
 
 P = 128
 PACK = 4
@@ -20,6 +21,7 @@ GROUP = 16
 SPARE = 192
 CHUNKS = ((0, 128), (128, 256), (256, 384), (384, 512))
 HALVES = ((0, 256), (256, 512))
+LAST_PIECES = ((0, 256), (256, 384), (384, 512))
 
 
 def tile_picked_yfmm_tanh_p_kernel(
@@ -40,9 +42,9 @@ def tile_picked_yfmm_tanh_p_kernel(
         def entries(tile, lo, hi):
             return tile[:, lo // GROUP : hi // GROUP]
 
-        def quantize(values, name, tag):
+        def quantize(values, name):
             width = values.shape[1] // PACK
-            codes = keep.tile([P, width], U32, name=name + "_codes", tag=tag, align_bytes=64)
+            codes = keep.tile([P, width], U32, name=name + "_codes", align_bytes=64)
             scales = keep.tile([P, width], U8, name=name + "_scales", align_bytes=64)
             nc.vector.quantize_mx(out=codes[:].bitcast(FP8X4), scales=scales[:], in_=values)
             return codes, scales
@@ -54,7 +56,6 @@ def tile_picked_yfmm_tanh_p_kernel(
         nc.vector.memset(x_bytes[32:64, :].bitcast(I32), 0)
         nc.vector.memset(x_bytes[64:P, :].bitcast(I32), 0)
         offs_sb = load_list(offs, "offs_sb")
-        close_sb = load_list(close, "close_sb")
         x_table = keep.tile([P, T], I32, name="x_table", align_bytes=64)
         nc.sync.dma_start(x_table[:], x_words[0].rearrange("p c r -> p (c r)").bitcast(I32))
         w1_rows = w1.rearrange("(p j) c -> p j c", j=PACK)
@@ -64,44 +65,32 @@ def tile_picked_yfmm_tanh_p_kernel(
         ]
         for half in range(2):
             nc.sync.dma_start(w1_raw[half][:], w1_rows[:, :, half * (H // 2) : (half + 1) * (H // 2)])
-
+        close_sb = load_list(close, "close_sb")
         far1_sb = load_list(far1, "far1_sb")
         far2_sb = load_list(far2, "far2_sb")
         far3_sb = load_list(far3, "far3_sb")
 
-        h = keep.tile([P, PACK * V + SPARE], F32, name="h", align_bytes=64)
-        nc.vector.memset(h[:, PACK * V : PACK * V + SPARE // 2], 0.0)
-        nc.scalar.copy(h[:, PACK * V + SPARE // 2 :], h[:, PACK * V : PACK * V + SPARE // 2])
+        h = [keep.tile([P, V + SPARE], F32, name="h%d" % t, align_bytes=64) for t in range(PACK)]
+        nc.vector.memset(h[0][:, V:], 0.0)
+        for t in range(1, PACK):
+            nc.scalar.activation(h[t][:, V:], h[0][:, V:], COPY)
 
-        def plane(t, lo, hi):
-            base = (PACK - 1 - t) * V
-            return h[:, base + lo : base + hi]
-
-        pick_bytes = keep.tile([P, S], U8, name="pick_bytes", align_bytes=64)
-        for lo, hi in HALVES:
-            nc.vector.tensor_copy(pick_bytes[:, D * lo : D * hi], x_bytes[:].indirect(entries(offs_sb, D * lo, D * hi)))
-        close_words = keep.tile([P, V], U32, name="close_words", align_bytes=64)
-        nc.vector.tensor_copy(close_words[:], x_table[:].bitcast(U32).indirect(close_sb[:]))
-        pair_words = keep.tile([P, D, V], U32, name="pair_words", tag="pair_words", align_bytes=64)
+        pick_tile = early.tile([P, 17 * V], U8, name="pick_bytes", offset=0, align_bytes=64)
+        pick_bytes = pick_tile[:, :S]
+        nc.vector.tensor_copy(pick_bytes.rearrange("p (d v) -> p v d", d=D), x_bytes[:].indirect(offs_sb[:]))
+        pair_words = keep.tile([P, D, V], U32, name="pair_words", align_bytes=64)
         nc.vector.tensor_copy(pair_words[:].rearrange("p d v -> p v d"), x_table[:].bitcast(U32).indirect(offs_sb[:]))
-        parted_tile = early.tile([P, 17 * V], U8, name="parted", offset=0, align_bytes=64)
-        parted = parted_tile[:, :S]
-        for lo, hi in HALVES:
-            nc.vector.tensor_copy(
-                parted.rearrange("p (d v) -> p d v", d=D)[:, :, lo:hi],
-                pick_bytes[:, D * lo : D * hi].rearrange("p (v d) -> p d v", d=D),
-            )
 
         def place_rows(dst, src, first, queue):
             for r in range(4):
                 queue.dma_start(dst[r:P:32, :].bitcast(I32), src[2 * r + first : 32 : 8, :].bitcast(I32))
 
-        pair_flat = keep.tile([P, S], U8, name="pair_bytes", tag="stage_b", align_bytes=64)
-        place_rows(pair_flat, parted, 0, nc.scalar)
+        pair_flat = keep.tile([P, S], U8, name="pair_bytes", align_bytes=64)
+        place_rows(pair_flat, pick_bytes, 0, nc.scalar)
         pair_bytes = pair_flat[:].rearrange("p (d v) -> p d v", d=D)
 
         small_raw = []
-        for i, mat in enumerate((w2, t1, t2, t3)):
+        for i, mat in enumerate((w2, t1, t3, t2)):
             raw = early.tile([P, PACK, N], F32, name="small_raw%d" % i, offset=4 * V * i, align_bytes=64)
             nc.sync.dma_start(raw[:], mat.rearrange("(p j) n -> p j n", j=PACK))
             small_raw.append(raw)
@@ -114,29 +103,17 @@ def tile_picked_yfmm_tanh_p_kernel(
             src = w1_raw[half][:].rearrange("p j (m t) -> p m j t", t=PACK)
             for u in range(2):
                 nc.scalar.copy(w1_bf[u][:, :, ms, :].rearrange("p t m j -> p m j t"), src[:, :, :, 2 * u : 2 * u + 2])
-        w1_mx = [
-            quantize(w1_bf[0][:, t].rearrange("p m j -> p (m j)"), "w1_%d" % t, "w1_plane%d" % t) for t in range(2)
-        ]
-        codes, scales = quantize(w1_bf[1][:].rearrange("p t m j -> p (t m j)"), "w1_23", "w1_codes1")
+        w1_mx = [quantize(w1_bf[0][:, t].rearrange("p m j -> p (m j)"), "w1_%d" % t) for t in range(2)]
+        codes, scales = quantize(w1_bf[1][:].rearrange("p t m j -> p (t m j)"), "w1_23")
         for t in range(2):
             w1_mx.append((codes[:, t * P : (t + 1) * P], scales[:, t * P : (t + 1) * P]))
 
         close_picked = late.tile([P, V], U8, name="close_picked", offset=0, align_bytes=64)
         nc.vector.tensor_copy(close_picked[:], x_bytes[:].indirect(close_sb[:]))
+        close_words = late.tile([P, V], U32, name="close_words", offset=V, align_bytes=64)
+        nc.vector.tensor_copy(close_words[:], x_table[:].bitcast(U32).indirect(close_sb[:]))
         close_bytes = keep.tile([P, V], U8, name="close_bytes", align_bytes=64)
         place_rows(close_bytes, close_picked, 1, nc.sync)
-
-        warm = psum.tile([P, V], F32, name="warm", tag="h_bank3")
-        for i in range(3):
-            nc.tensor.matmul_mx(
-                out=warm[:],
-                lhsT=close_words[:, :P].bitcast(FP8X4),
-                lhsT_scale=parted[:, :P],
-                rhs=close_words[:].bitcast(FP8X4),
-                rhs_scale=parted[:, :V],
-                start=True,
-                stop=True,
-            )
 
         def moments(t, bank, lo, hi):
             for d in range(D):
@@ -150,91 +127,68 @@ def tile_picked_yfmm_tanh_p_kernel(
                     stop=(d == D - 1),
                 )
 
-        pieces = [(0, HALVES[0]), (0, CHUNKS[2]), (0, CHUNKS[3]), (1, HALVES[0]), (1, HALVES[1])]
-        for i, (t, (lo, hi)) in enumerate(pieces):
-            bank = psum.tile([P, hi - lo], F32, name="h_piece", tag="bank%d" % i)
-            moments(t, bank[:], lo, hi)
-            nc.scalar.copy(plane(t, lo, hi), bank[:])
-        for t in range(2, PACK):
-            bank = psum.tile([P, V], F32, name="h_bank%d" % t, tag="h_bank%d" % t)
-            moments(t, bank[:], 0, V)
-            nc.scalar.copy(plane(t, 0, V), bank[:])
+        m0 = keep.tile([P, PACK, V], F32, name="m0", align_bytes=64)
+        m1 = keep.tile([P, PACK, V], F32, name="m1", align_bytes=64)
+        m2 = keep.tile([P, PACK, V], F32, name="m2", align_bytes=64)
+        for t in range(PACK):
+            pieces = HALVES if t == 0 else ((0, V),)
+            for i, (lo, hi) in enumerate(pieces):
+                bank = psum.tile([P, hi - lo], F32, name="h_bank", tag="bank%d" % i if t == 0 else "h_bank%d" % t)
+                moments(t, bank[:], lo, hi)
+                nc.scalar.copy(h[t][:, lo:hi], bank[:])
+            nc.scalar.activation(m0[:, t, :], h[t][:].indirect(far1_sb[:]), COPY)
+        nc.scalar.activation(m2[:, PACK - 1, :], h[PACK - 1][:].indirect(far3_sb[:]), COPY)
+        for lo, hi in LAST_PIECES:
+            for t in range(PACK):
+                nc.scalar.activation(m1[:, t, lo:hi], h[t][:].indirect(entries(far2_sb, lo, hi)), COPY)
 
-        small_bf = []
-        for u, tag in enumerate(("pair_words", "w1_codes1")):
-            rounded = keep.tile([P, 2, N, PACK], BF16, name="small_bf%d" % u, tag=tag, align_bytes=64)
-            for i in range(2):
-                nc.scalar.copy(
-                    rounded[:, i].rearrange("p (c e) j -> p c j e", e=4),
-                    small_raw[2 * u + i][:].rearrange("p j (c e) -> p c j e", e=4),
-                )
-            small_bf.append(rounded[:].rearrange("p i n j -> p (i n j)"))
-        codes, scales = quantize(small_bf[0], "small0", "small0_codes")
-        small = [(codes[:, i * N : (i + 1) * N], scales[:, i * N : (i + 1) * N]) for i in range(2)]
+        def weave(fetched, woven):
+            nc.vector.tensor_copy(
+                woven.rearrange("p (c e) t -> p c t e", e=4), fetched.rearrange("p t (c e) -> p c t e", e=4)
+            )
+
+        small_bf = keep.tile([P, 4, N, PACK], BF16, name="small_bf", align_bytes=64)
+        for i in range(4):
+            weave(small_raw[i][:], small_bf[:, i])
+        for t in range(PACK - 1):
+            nc.vector.tensor_copy(m2[:, t, :], h[t][:].indirect(far3_sb[:]))
+        codes, scales = quantize(small_bf[:].rearrange("p i n j -> p (i n j)"), "small")
+        small = [(codes[:, i * N : (i + 1) * N], scales[:, i * N : (i + 1) * N]) for i in range(4)]
 
         banks = [psum.tile([P, hi - lo], F32, name="out_bank%d" % c, tag="bank%d" % c) for c, (lo, hi) in enumerate(CHUNKS)]
 
         def product(i, c, codes, scales):
             nc.tensor.matmul_mx(
                 out=banks[c][:],
-                lhsT=small[i][0][:, :].bitcast(FP8X4),
-                lhsT_scale=small[i][1][:, :],
+                lhsT=small[i][0].bitcast(FP8X4),
+                lhsT_scale=small[i][1],
                 rhs=codes.bitcast(FP8X4),
                 rhs_scale=scales,
                 start=(i == 0),
                 stop=(i == 3),
             )
 
-        def weave(fetched, name):
-            width = fetched.shape[2]
-            woven = keep.tile([P, width, PACK], BF16, name=name, tag=name, align_bytes=64)
-            nc.scalar.copy(
-                woven[:].rearrange("p (c e) t -> p c t e", e=4), fetched.rearrange("p t (c e) -> p c t e", e=4)
-            )
-            return woven[:].rearrange("p c t -> p (c t)")
-
         for c, (lo, hi) in enumerate(CHUNKS):
             product(0, c, close_words[:, lo:hi], close_bytes[:, lo:hi])
 
-        m0 = late.tile([P, PACK + 1, V], F32, name="m0", offset=8 * V, align_bytes=64)
-        for t in range(PACK):
-            nc.vector.tensor_copy(m0[:, t, :], plane(t, 0, V + SPARE).indirect(far1_sb[:]))
-        m1 = keep.tile([P, PACK, V], F32, name="m1", tag="stage_b", align_bytes=64)
-        for t in range(PACK):
-            nc.vector.tensor_copy(m1[:, t, :], plane(t, 0, V + SPARE).indirect(far2_sb[:]))
+        steps = [(1, m0, 0, V), (2, m2, 0, V)] + [(3, m1, lo, hi) for lo, hi in LAST_PIECES]
+        woven = []
+        for i, m, lo, hi in steps:
+            woven.append(keep.tile([P, hi - lo, PACK], BF16, name="woven%d_%d" % (i, lo), align_bytes=64))
 
-        half = V // 2
+        def finish(step):
+            i, m, lo, hi = steps[step]
+            codes, scales = quantize(woven[step][:].rearrange("p c t -> p (c t)"), "m%d_%d" % (i, lo))
+            for c, (a, b) in enumerate(CHUNKS):
+                if lo <= a and b <= hi:
+                    product(i, c, codes[:, a - lo : b - lo], scales[:, a - lo : b - lo])
+                    if i == 3:
+                        result = keep.tile([P, b - a], F32, name="result%d" % c)
+                        nc.scalar.activation(result[:], banks[c][:], TANH, bias=bias_sb[:])
+                        nc.sync.dma_start(out[:, a:b], result[:])
 
-        def far_half(i, u, woven):
-            codes, scales = quantize(woven, "m%dq%d" % (i, u), "m%d_codes%d" % (i, u))
-            for c in (2 * u, 2 * u + 1):
-                lo, hi = CHUNKS[c]
-                product(i + 1, c, codes[:, lo % half : lo % half + hi - lo], scales[:, lo % half : lo % half + hi - lo])
-
-        m0_woven = [weave(m0[:, :PACK, lo:hi], "m0_woven%d" % u) for u, (lo, hi) in enumerate(HALVES)]
-        far_half(0, 0, m0_woven[0])
-
-        m2 = late.tile([P, PACK, V], F32, name="m2", offset=8 * V, align_bytes=64)
-        for t in range(2):
-            nc.vector.tensor_copy(m2[:, t, :], plane(t, 0, V + SPARE).indirect(far3_sb[:]))
-        for lo, hi in HALVES:
-            for t in range(2, PACK):
-                nc.vector.tensor_copy(m2[:, t, lo:hi], plane(t, 0, V).indirect(entries(far3_sb, lo, hi)))
-        far_half(0, 1, m0_woven[1])
-        codes = late.tile([P, N], U32, name="t2_codes", offset=24 * V, align_bytes=64)
-        scales = keep.tile([P, N], U8, name="t2_scales", align_bytes=64)
-        nc.vector.quantize_mx(out=codes[:].bitcast(FP8X4), scales=scales[:], in_=small_bf[1][:, : PACK * N])
-        small.append((codes, scales))
-
-        m1_woven = [weave(m1[:, :, lo:hi], "m1_woven%d" % u) for u, (lo, hi) in enumerate(HALVES)]
-        m2_woven = [weave(m2[:, :, lo:hi], "m2_woven%d" % c) for c, (lo, hi) in enumerate(CHUNKS)]
-
-        for u in range(2):
-            far_half(1, u, m1_woven[u])
-        small.append(quantize(small_bf[1][:, PACK * N :], "t3", "stage_b"))
-        for c, (lo, hi) in enumerate(CHUNKS):
-            codes, scales = quantize(m2_woven[c], "m2q%d" % c, "m2_codes%d" % c)
-            product(3, c, codes[:], scales[:])
-            result = keep.tile([P, hi - lo], F32, name="result%d" % c)
-            nc.scalar.activation(result[:], banks[c][:], TANH, bias=bias_sb[:])
-            nc.sync.dma_start(out[:, lo:hi], result[:])
+        for step, (i, m, lo, hi) in enumerate(steps):
+            weave(m[:, :, lo:hi], woven[step][:])
+            if step > 0:
+                finish(step - 1)
+        finish(len(steps) - 1)

@@ -20,7 +20,6 @@ PACK = 4
 GROUP = 16
 SPARE = 192
 CHUNKS = ((0, 128), (128, 256), (256, 384), (384, 512))
-HALVES = ((0, 256), (256, 512))
 LAST_PIECES = ((0, 256), (256, 384), (384, 512))
 
 
@@ -56,6 +55,8 @@ def tile_picked_yfmm_tanh_p_kernel(
         nc.vector.memset(x_bytes[32:64, :].bitcast(I32), 0)
         nc.vector.memset(x_bytes[64:P, :].bitcast(I32), 0)
         offs_sb = load_list(offs, "offs_sb")
+        close_sb = load_list(close, "close_sb")
+        far1_sb = load_list(far1, "far1_sb")
         x_table = keep.tile([P, T], I32, name="x_table", align_bytes=64)
         nc.sync.dma_start(x_table[:], x_words[0].rearrange("p c r -> p (c r)").bitcast(I32))
         w1_rows = w1.rearrange("(p j) c -> p j c", j=PACK)
@@ -65,8 +66,6 @@ def tile_picked_yfmm_tanh_p_kernel(
         ]
         for half in range(2):
             nc.sync.dma_start(w1_raw[half][:], w1_rows[:, :, half * (H // 2) : (half + 1) * (H // 2)])
-        close_sb = load_list(close, "close_sb")
-        far1_sb = load_list(far1, "far1_sb")
         far2_sb = load_list(far2, "far2_sb")
         far3_sb = load_list(far3, "far3_sb")
 
@@ -80,6 +79,8 @@ def tile_picked_yfmm_tanh_p_kernel(
         nc.vector.tensor_copy(pick_bytes.rearrange("p (d v) -> p v d", d=D), x_bytes[:].indirect(offs_sb[:]))
         pair_words = keep.tile([P, D, V], U32, name="pair_words", align_bytes=64)
         nc.vector.tensor_copy(pair_words[:].rearrange("p d v -> p v d"), x_table[:].bitcast(U32).indirect(offs_sb[:]))
+        close_first = keep.tile([P, V // 2], U32, name="close_first", align_bytes=64)
+        nc.vector.tensor_copy(close_first[:], x_table[:].bitcast(U32).indirect(entries(close_sb, 0, V // 2)))
 
         def place_rows(dst, src, first, queue):
             for r in range(4):
@@ -110,8 +111,9 @@ def tile_picked_yfmm_tanh_p_kernel(
 
         close_picked = late.tile([P, V], U8, name="close_picked", offset=0, align_bytes=64)
         nc.vector.tensor_copy(close_picked[:], x_bytes[:].indirect(close_sb[:]))
-        close_words = late.tile([P, V], U32, name="close_words", offset=V, align_bytes=64)
-        nc.vector.tensor_copy(close_words[:], x_table[:].bitcast(U32).indirect(close_sb[:]))
+        close_second = late.tile([P, V // 2], U32, name="close_second", offset=V, align_bytes=64)
+        nc.vector.tensor_copy(close_second[:], x_table[:].bitcast(U32).indirect(entries(close_sb, V // 2, V)))
+        close_words = [close_first, close_second]
         close_bytes = keep.tile([P, V], U8, name="close_bytes", align_bytes=64)
         place_rows(close_bytes, close_picked, 1, nc.sync)
 
@@ -131,7 +133,7 @@ def tile_picked_yfmm_tanh_p_kernel(
         m1 = keep.tile([P, PACK, V], F32, name="m1", align_bytes=64)
         m2 = keep.tile([P, PACK, V], F32, name="m2", align_bytes=64)
         for t in range(PACK):
-            pieces = HALVES if t == 0 else ((0, V),)
+            pieces = LAST_PIECES if t == 0 else ((0, V),)
             for i, (lo, hi) in enumerate(pieces):
                 bank = psum.tile([P, hi - lo], F32, name="h_bank", tag="bank%d" % i if t == 0 else "h_bank%d" % t)
                 moments(t, bank[:], lo, hi)
@@ -144,7 +146,7 @@ def tile_picked_yfmm_tanh_p_kernel(
 
         def weave(fetched, woven):
             nc.vector.tensor_copy(
-                woven.rearrange("p (c e) t -> p c t e", e=4), fetched.rearrange("p t (c e) -> p c t e", e=4)
+                woven.rearrange("p (c e) t -> p c t e", e=2), fetched.rearrange("p t (c e) -> p c t e", e=2)
             )
 
         small_bf = keep.tile([P, 4, N, PACK], BF16, name="small_bf", align_bytes=64)
@@ -169,7 +171,7 @@ def tile_picked_yfmm_tanh_p_kernel(
             )
 
         for c, (lo, hi) in enumerate(CHUNKS):
-            product(0, c, close_words[:, lo:hi], close_bytes[:, lo:hi])
+            product(0, c, close_words[c // 2][:, lo % 256 : lo % 256 + hi - lo], close_bytes[:, lo:hi])
 
         steps = [(1, m0, 0, V), (2, m2, 0, V)] + [(3, m1, lo, hi) for lo, hi in LAST_PIECES]
         woven = []

@@ -139,7 +139,6 @@ def tile_picked_yfmm_tanh_p_kernel(
                 moments(t, bank[:], lo, hi)
                 nc.scalar.copy(h[t][:, lo:hi], bank[:])
             nc.scalar.activation(m0[:, t, :], h[t][:].indirect(far1_sb[:]), COPY)
-        nc.scalar.activation(m2[:, PACK - 1, :], h[PACK - 1][:].indirect(far3_sb[:]), COPY)
         for lo, hi in LAST_PIECES:
             for t in range(PACK):
                 nc.scalar.activation(m1[:, t, lo:hi], h[t][:].indirect(entries(far2_sb, lo, hi)), COPY)
@@ -152,7 +151,7 @@ def tile_picked_yfmm_tanh_p_kernel(
         small_bf = keep.tile([P, 4, N, PACK], BF16, name="small_bf", align_bytes=64)
         for i in range(4):
             weave(small_raw[i][:], small_bf[:, i])
-        for t in range(PACK - 1):
+        for t in range(PACK):
             nc.vector.tensor_copy(m2[:, t, :], h[t][:].indirect(far3_sb[:]))
         codes, scales = quantize(small_bf[:].rearrange("p i n j -> p (i n j)"), "small")
         small = [(codes[:, i * N : (i + 1) * N], scales[:, i * N : (i + 1) * N]) for i in range(4)]

@@ -13,6 +13,8 @@ U16 = mybir.dt.uint16
 U8 = mybir.dt.uint8
 FP8X4 = mybir.dt.float8_e4m3fn_x4
 TANH = mybir.ActivationFunctionType.Tanh
+MULT = mybir.AluOpType.mult
+ADD = mybir.AluOpType.add
 COPY = mybir.ActivationFunctionType.Copy
 
 P = 128
@@ -130,18 +132,21 @@ def tile_picked_yfmm_tanh_p_kernel(
                 )
 
         m0 = keep.tile([P, PACK, V], F32, name="m0", align_bytes=64)
-        m1 = keep.tile([P, PACK, V], F32, name="m1", align_bytes=64)
+        m1 = [keep.tile([P, PACK, hi - lo], F32, name="m1_%d" % lo, align_bytes=64) for lo, hi in LAST_PIECES]
         m2 = keep.tile([P, PACK, V], F32, name="m2", align_bytes=64)
         for t in range(PACK):
             pieces = LAST_PIECES if t == 0 else ((0, V),)
             for i, (lo, hi) in enumerate(pieces):
                 bank = psum.tile([P, hi - lo], F32, name="h_bank", tag="bank%d" % i if t == 0 else "h_bank%d" % t)
                 moments(t, bank[:], lo, hi)
-                nc.scalar.copy(h[t][:, lo:hi], bank[:])
+                if t < 2:
+                    nc.scalar.copy(h[t][:, lo:hi], bank[:])
+                else:
+                    nc.vector.tensor_copy(h[t][:, lo:hi], bank[:])
             nc.scalar.activation(m0[:, t, :], h[t][:].indirect(far1_sb[:]), COPY)
-        for lo, hi in LAST_PIECES:
+        for piece, (lo, hi) in zip(m1, LAST_PIECES):
             for t in range(PACK):
-                nc.scalar.activation(m1[:, t, lo:hi], h[t][:].indirect(entries(far2_sb, lo, hi)), COPY)
+                nc.scalar.activation(piece[:, t, :], h[t][:].indirect(entries(far2_sb, lo, hi)), COPY)
 
         def weave(fetched, woven):
             nc.vector.tensor_copy(
@@ -150,7 +155,14 @@ def tile_picked_yfmm_tanh_p_kernel(
 
         small_bf = keep.tile([P, 4, N, PACK], BF16, name="small_bf", align_bytes=64)
         for i in range(4):
-            weave(small_raw[i][:], small_bf[:, i])
+            nc.gpsimd.tensor_scalar(
+                small_bf[:, i].rearrange("p (c e) j -> p c j e", e=2),
+                small_raw[i][:].rearrange("p j (c e) -> p c j e", e=2),
+                1.0,
+                0.0,
+                MULT,
+                ADD,
+            )
         for t in range(PACK):
             nc.vector.tensor_copy(m2[:, t, :], h[t][:].indirect(far3_sb[:]))
         codes, scales = quantize(small_bf[:].rearrange("p i n j -> p (i n j)"), "small")
@@ -172,7 +184,7 @@ def tile_picked_yfmm_tanh_p_kernel(
         for c, (lo, hi) in enumerate(CHUNKS):
             product(0, c, close_words[c // 2][:, lo % 256 : lo % 256 + hi - lo], close_bytes[:, lo:hi])
 
-        steps = [(1, m0, 0, V), (2, m2, 0, V)] + [(3, m1, lo, hi) for lo, hi in LAST_PIECES]
+        steps = [(1, m0, 0, V), (2, m2, 0, V)] + [(3, piece, lo, hi) for piece, (lo, hi) in zip(m1, LAST_PIECES)]
         woven = []
         for i, m, lo, hi in steps:
             woven.append(keep.tile([P, hi - lo, PACK], BF16, name="woven%d_%d" % (i, lo), align_bytes=64))
@@ -189,7 +201,7 @@ def tile_picked_yfmm_tanh_p_kernel(
                         nc.sync.dma_start(out[:, a:b], result[:])
 
         for step, (i, m, lo, hi) in enumerate(steps):
-            weave(m[:, :, lo:hi], woven[step][:])
+            weave(m[:], woven[step][:])
             if step > 0:
                 finish(step - 1)
         finish(len(steps) - 1)

@@ -93,7 +93,7 @@ def tile_picked_yfmm_tanh_p_kernel(
         pair_bytes = pair_flat[:].rearrange("p (d v) -> p d v", d=D)
 
         small_raw = []
-        for i, mat in enumerate((w2, t1, t3, t2)):
+        for i, mat in enumerate((w2, t3, t1, t2)):
             raw = early.tile([P, PACK, N], F32, name="small_raw%d" % i, offset=4 * V * i, align_bytes=64)
             nc.sync.dma_start(raw[:], mat.rearrange("(p j) n -> p j n", j=PACK))
             small_raw.append(raw)
@@ -133,7 +133,7 @@ def tile_picked_yfmm_tanh_p_kernel(
 
         m0 = keep.tile([P, PACK, V], F32, name="m0", align_bytes=64)
         m1 = [keep.tile([P, PACK, hi - lo], F32, name="m1_%d" % lo, align_bytes=64) for lo, hi in LAST_PIECES]
-        m2 = keep.tile([P, PACK, V], F32, name="m2", align_bytes=64)
+        m2 = keep.tile([P, 2, V, 2], BF16, name="m2", align_bytes=64)
         for t in range(PACK):
             pieces = LAST_PIECES if t == 0 else ((0, V),)
             for i, (lo, hi) in enumerate(pieces):
@@ -156,15 +156,15 @@ def tile_picked_yfmm_tanh_p_kernel(
         small_bf = keep.tile([P, 4, N, PACK], BF16, name="small_bf", align_bytes=64)
         for i in range(4):
             nc.gpsimd.tensor_scalar(
-                small_bf[:, i].rearrange("p (c e) j -> p c j e", e=2),
-                small_raw[i][:].rearrange("p j (c e) -> p c j e", e=2),
+                small_bf[:, i],
+                small_raw[i][:].rearrange("p j n -> p n j"),
                 1.0,
                 0.0,
                 MULT,
                 ADD,
             )
         for t in range(PACK):
-            nc.vector.tensor_copy(m2[:, t, :], h[t][:].indirect(far3_sb[:]))
+            nc.vector.tensor_copy(m2[:, t // 2, :, t % 2], h[t][:].indirect(far3_sb[:]))
         codes, scales = quantize(small_bf[:].rearrange("p i n j -> p (i n j)"), "small")
         small = [(codes[:, i * N : (i + 1) * N], scales[:, i * N : (i + 1) * N]) for i in range(4)]
 
@@ -184,7 +184,7 @@ def tile_picked_yfmm_tanh_p_kernel(
         for c, (lo, hi) in enumerate(CHUNKS):
             product(0, c, close_words[c // 2][:, lo % 256 : lo % 256 + hi - lo], close_bytes[:, lo:hi])
 
-        steps = [(1, m0, 0, V), (2, m2, 0, V)] + [(3, piece, lo, hi) for piece, (lo, hi) in zip(m1, LAST_PIECES)]
+        steps = [(1, m2, 0, V), (2, m0, 0, V)] + [(3, piece, lo, hi) for piece, (lo, hi) in zip(m1, LAST_PIECES)]
         woven = []
         for i, m, lo, hi in steps:
             woven.append(keep.tile([P, hi - lo, PACK], BF16, name="woven%d_%d" % (i, lo), align_bytes=64))
@@ -200,8 +200,11 @@ def tile_picked_yfmm_tanh_p_kernel(
                         nc.scalar.activation(result[:], banks[c][:], TANH, bias=bias_sb[:])
                         nc.sync.dma_start(out[:, a:b], result[:])
 
-        for step, (i, m, lo, hi) in enumerate(steps):
-            weave(m[:], woven[step][:])
-            if step > 0:
-                finish(step - 1)
+        nc.vector.tensor_copy(
+            woven[0][:].rearrange("p v t -> p (v t)").bitcast(I32).rearrange("p (c e u) -> p c u e", e=2, u=2),
+            m2[:].rearrange("p u v s -> p (u v s)").bitcast(I32).rearrange("p (u c e) -> p c u e", e=2, u=2),
+        )
+        for step in range(1, len(steps)):
+            weave(steps[step][1][:], woven[step][:])
+            finish(step - 1)
         finish(len(steps) - 1)

@@ -13,16 +13,16 @@ U16 = mybir.dt.uint16
 U8 = mybir.dt.uint8
 FP8X4 = mybir.dt.float8_e4m3fn_x4
 TANH = mybir.ActivationFunctionType.Tanh
+COPY = mybir.ActivationFunctionType.Copy
 MULT = mybir.AluOpType.mult
 ADD = mybir.AluOpType.add
-COPY = mybir.ActivationFunctionType.Copy
 
 P = 128
 PACK = 4
 GROUP = 16
-SPARE = 192
+ROW = 2 * V
 CHUNKS = ((0, 128), (128, 256), (256, 384), (384, 512))
-LAST_PIECES = ((0, 256), (256, 384), (384, 512))
+PIECES = ((0, 256), (256, 384), (384, 512))
 
 
 def tile_picked_yfmm_tanh_p_kernel(
@@ -33,6 +33,8 @@ def tile_picked_yfmm_tanh_p_kernel(
         keep = ctx.enter_context(tc.tile_pool(name="keep", bufs=1))
         late = ctx.enter_context(tc.tile_pool(name="late", bufs=1))
         early = ctx.enter_context(tc.tile_pool(name="early", bufs=1))
+        mid = ctx.enter_context(tc.tile_pool(name="mid", bufs=1))
+        last = ctx.enter_context(tc.tile_pool(name="last", bufs=1))
         psum = ctx.enter_context(tc.psum_pool(name="psum", bufs=1))
 
         def load_list(src, name):
@@ -43,10 +45,12 @@ def tile_picked_yfmm_tanh_p_kernel(
         def entries(tile, lo, hi):
             return tile[:, lo // GROUP : hi // GROUP]
 
-        def quantize(values, name):
+        def quantize(values, name, codes=None, scales=None):
             width = values.shape[1] // PACK
-            codes = keep.tile([P, width], U32, name=name + "_codes", align_bytes=64)
-            scales = keep.tile([P, width], U8, name=name + "_scales", align_bytes=64)
+            if codes is None:
+                codes = keep.tile([P, width], U32, name=name + "_codes", align_bytes=64)
+            if scales is None:
+                scales = keep.tile([P, width], U8, name=name + "_scales", align_bytes=64)
             nc.vector.quantize_mx(out=codes[:].bitcast(FP8X4), scales=scales[:], in_=values)
             return codes, scales
 
@@ -71,12 +75,15 @@ def tile_picked_yfmm_tanh_p_kernel(
         far2_sb = load_list(far2, "far2_sb")
         far3_sb = load_list(far3, "far3_sb")
 
-        h = [keep.tile([P, V + SPARE], F32, name="h%d" % t, align_bytes=64) for t in range(PACK)]
-        nc.vector.memset(h[0][:, V:], 0.0)
+        h = keep.tile([P, PACK * ROW], F32, name="h", align_bytes=64)
+        nc.vector.memset(h[:, V:ROW], 0.0)
         for t in range(1, PACK):
-            nc.scalar.activation(h[t][:, V:], h[0][:, V:], COPY)
+            nc.scalar.activation(h[:, t * ROW + V : (t + 1) * ROW], h[:, V:ROW], COPY)
 
-        pick_tile = early.tile([P, 17 * V], U8, name="pick_bytes", offset=0, align_bytes=64)
+        def window(t, to_end):
+            return h[:, t * ROW : (PACK if to_end else t + 1) * ROW]
+
+        pick_tile = early.tile([P, 64 + 16 * V], U8, name="pick_bytes", offset=0, align_bytes=64)
         pick_bytes = pick_tile[:, :S]
         nc.vector.tensor_copy(pick_bytes.rearrange("p (d v) -> p v d", d=D), x_bytes[:].indirect(offs_sb[:]))
         pair_words = keep.tile([P, D, V], U32, name="pair_words", align_bytes=64)
@@ -93,11 +100,11 @@ def tile_picked_yfmm_tanh_p_kernel(
         pair_bytes = pair_flat[:].rearrange("p (d v) -> p d v", d=D)
 
         small_raw = []
-        for i, mat in enumerate((w2, t3, t1, t2)):
-            raw = early.tile([P, PACK, N], F32, name="small_raw%d" % i, offset=4 * V * i, align_bytes=64)
+        for i, mat in enumerate((w2, t1, t3, t2)):
+            raw = early.tile([P, PACK, N], F32, name="small_raw%d" % i, offset=64 + 4 * V * i, align_bytes=64)
             nc.sync.dma_start(raw[:], mat.rearrange("(p j) n -> p j n", j=PACK))
             small_raw.append(raw)
-        bias_sb = early.tile([P, 1], F32, name="bias_sb", offset=16 * V, align_bytes=64)
+        bias_sb = early.tile([P, 1], F32, name="bias_sb", offset=0, align_bytes=64)
         nc.sync.dma_start(bias_sb[:], bias)
 
         w1_bf = [keep.tile([P, 2, P, PACK], BF16, name="w1_bf%d" % u, align_bytes=64) for u in range(2)]
@@ -107,15 +114,13 @@ def tile_picked_yfmm_tanh_p_kernel(
             for u in range(2):
                 nc.scalar.copy(w1_bf[u][:, :, ms, :].rearrange("p t m j -> p m j t"), src[:, :, :, 2 * u : 2 * u + 2])
         w1_mx = [quantize(w1_bf[0][:, t].rearrange("p m j -> p (m j)"), "w1_%d" % t) for t in range(2)]
-        codes, scales = quantize(w1_bf[1][:].rearrange("p t m j -> p (t m j)"), "w1_23")
+        codes = mid.tile([P, 2 * P], U32, name="w1_23_codes", offset=0, align_bytes=64)
+        codes, scales = quantize(w1_bf[1][:].rearrange("p t m j -> p (t m j)"), "w1_23", codes=codes)
         for t in range(2):
             w1_mx.append((codes[:, t * P : (t + 1) * P], scales[:, t * P : (t + 1) * P]))
 
         close_picked = late.tile([P, V], U8, name="close_picked", offset=0, align_bytes=64)
         nc.vector.tensor_copy(close_picked[:], x_bytes[:].indirect(close_sb[:]))
-        close_second = late.tile([P, V // 2], U32, name="close_second", offset=V, align_bytes=64)
-        nc.vector.tensor_copy(close_second[:], x_table[:].bitcast(U32).indirect(entries(close_sb, V // 2, V)))
-        close_words = [close_first, close_second]
         close_bytes = keep.tile([P, V], U8, name="close_bytes", align_bytes=64)
         place_rows(close_bytes, close_picked, 1, nc.sync)
 
@@ -131,41 +136,58 @@ def tile_picked_yfmm_tanh_p_kernel(
                     stop=(d == D - 1),
                 )
 
-        m0 = keep.tile([P, PACK, V], F32, name="m0", align_bytes=64)
-        m1 = [keep.tile([P, PACK, hi - lo], F32, name="m1_%d" % lo, align_bytes=64) for lo, hi in LAST_PIECES]
+        m0 = last.tile([P, PACK, V], F32, name="m0", offset=8 * V - 64, align_bytes=64)
+        m1 = keep.tile([P, PACK, V], F32, name="m1", align_bytes=64)
         m2 = keep.tile([P, 2, V, 2], BF16, name="m2", align_bytes=64)
+
+        def fetch(m, far, t, lo, hi, to_end=True):
+            nc.scalar.activation(m[:, t, lo:hi], window(t, to_end).indirect(entries(far, lo, hi)), COPY)
+
         for t in range(PACK):
-            pieces = LAST_PIECES if t == 0 else ((0, V),)
+            pieces = PIECES if t == 0 else ((0, V),)
             for i, (lo, hi) in enumerate(pieces):
-                bank = psum.tile([P, hi - lo], F32, name="h_bank", tag="bank%d" % i if t == 0 else "h_bank%d" % t)
+                bank = psum.tile([P, hi - lo], F32, name="h_bank", tag="bank%d" % (i if t == 0 else (1, 3, 4)[t - 1]))
                 moments(t, bank[:], lo, hi)
                 if t < 2:
-                    nc.scalar.copy(h[t][:, lo:hi], bank[:])
+                    nc.scalar.copy(h[:, t * ROW + lo : t * ROW + hi], bank[:])
                 else:
-                    nc.vector.tensor_copy(h[t][:, lo:hi], bank[:])
-            nc.scalar.activation(m0[:, t, :], h[t][:].indirect(far1_sb[:]), COPY)
-        for piece, (lo, hi) in zip(m1, LAST_PIECES):
-            for t in range(PACK):
-                nc.scalar.activation(piece[:, t, :], h[t][:].indirect(entries(far2_sb, lo, hi)), COPY)
+                    nc.vector.tensor_copy(h[:, t * ROW + lo : t * ROW + hi], bank[:])
+            if t == 0:
+                fetch(m0, far1_sb, 0, 0, V // 2, False)
+                nc.vector.tensor_copy(m2[:, 0, :, 0], window(0, False).indirect(far3_sb[:]))
+        fetch(m0, far1_sb, 0, V // 2, V, False)
+        for t in (1, 2):
+            fetch(m0, far1_sb, t, 0, V // 2, False)
+        for t in (1, 2, 3):
+            fetch(m0, far1_sb, t, V // 2, V)
+        fetch(m1, far2_sb, 0, 0, V)
+        fetch(m1, far2_sb, 1, 0, V)
+        for lo, hi in PIECES:
+            for t in (2, 3):
+                fetch(m1, far2_sb, t, lo, hi)
 
-        def weave(fetched, woven):
-            nc.vector.tensor_copy(
-                woven.rearrange("p (c e) t -> p c t e", e=2), fetched.rearrange("p t (c e) -> p c t e", e=2)
-            )
+        close_second = mid.tile([P, V // 2], U32, name="close_second", offset=0, align_bytes=64)
+        nc.vector.tensor_copy(close_second[:], x_table[:].bitcast(U32).indirect(entries(close_sb, V // 2, V)))
+        close_words = [close_first, close_second]
+        nc.vector.tensor_copy(m0[:, 3, : V // 2], window(3, True).indirect(entries(far1_sb, 0, V // 2)))
+        for t in range(1, PACK):
+            nc.vector.tensor_copy(m2[:, t // 2, :, t % 2], window(t, True).indirect(far3_sb[:]))
 
         small_bf = keep.tile([P, 4, N, PACK], BF16, name="small_bf", align_bytes=64)
         for i in range(4):
-            nc.gpsimd.tensor_scalar(
-                small_bf[:, i],
-                small_raw[i][:].rearrange("p j n -> p n j"),
-                1.0,
-                0.0,
-                MULT,
-                ADD,
-            )
-        for t in range(PACK):
-            nc.vector.tensor_copy(m2[:, t // 2, :, t % 2], h[t][:].indirect(far3_sb[:]))
-        codes, scales = quantize(small_bf[:].rearrange("p i n j -> p (i n j)"), "small")
+            nc.gpsimd.tensor_scalar(small_bf[:, i], small_raw[i][:].rearrange("p j n -> p n j"), 1.0, 0.0, MULT, ADD)
+        woven0 = early.tile([P, V, PACK], BF16, name="woven0", offset=64 + 12 * V, align_bytes=64)
+        for lo, hi in ((0, V // 2), (V // 2, V)):
+            nc.gpsimd.tensor_scalar(woven0[:, lo:hi, :], m0[:, :, lo:hi].rearrange("p t v -> p v t"), 1.0, 0.0, MULT, ADD)
+
+        woven2 = last.tile([P, V, PACK], BF16, name="woven2", offset=0, align_bytes=64)
+        small_scales = last.tile([P, V], U8, name="small_scales", offset=8 * V, align_bytes=64)
+        woven1 = [
+            last.tile([P, hi - lo, PACK], BF16, name="woven1_%d" % lo, offset=9 * V + 8 * lo, align_bytes=64)
+            for lo, hi in PIECES
+        ]
+
+        codes, scales = quantize(small_bf[:].rearrange("p i n j -> p (i n j)"), "small", scales=small_scales)
         small = [(codes[:, i * N : (i + 1) * N], scales[:, i * N : (i + 1) * N]) for i in range(4)]
 
         banks = [psum.tile([P, hi - lo], F32, name="out_bank%d" % c, tag="bank%d" % c) for c, (lo, hi) in enumerate(CHUNKS)]
@@ -184,14 +206,8 @@ def tile_picked_yfmm_tanh_p_kernel(
         for c, (lo, hi) in enumerate(CHUNKS):
             product(0, c, close_words[c // 2][:, lo % 256 : lo % 256 + hi - lo], close_bytes[:, lo:hi])
 
-        steps = [(1, m2, 0, V), (2, m0, 0, V)] + [(3, piece, lo, hi) for piece, (lo, hi) in zip(m1, LAST_PIECES)]
-        woven = []
-        for i, m, lo, hi in steps:
-            woven.append(keep.tile([P, hi - lo, PACK], BF16, name="woven%d_%d" % (i, lo), align_bytes=64))
-
-        def finish(step):
-            i, m, lo, hi = steps[step]
-            codes, scales = quantize(woven[step][:].rearrange("p c t -> p (c t)"), "m%d_%d" % (i, lo))
+        def finish(i, woven, lo, hi):
+            codes, scales = quantize(woven[:].rearrange("p c t -> p (c t)"), "m%d_%d" % (i, lo))
             for c, (a, b) in enumerate(CHUNKS):
                 if lo <= a and b <= hi:
                     product(i, c, codes[:, a - lo : b - lo], scales[:, a - lo : b - lo])
@@ -200,11 +216,20 @@ def tile_picked_yfmm_tanh_p_kernel(
                         nc.scalar.activation(result[:], banks[c][:], TANH, bias=bias_sb[:])
                         nc.sync.dma_start(out[:, a:b], result[:])
 
+        def weave(k):
+            nc.vector.tensor_copy(
+                woven1[k][:].rearrange("p (c e) t -> p c t e", e=2), m1[:, :, PIECES[k][0] : PIECES[k][1]].rearrange("p t (c e) -> p c t e", e=2)
+            )
+
         nc.vector.tensor_copy(
-            woven[0][:].rearrange("p v t -> p (v t)").bitcast(I32).rearrange("p (c e u) -> p c u e", e=2, u=2),
+            woven2[:].rearrange("p v t -> p (v t)").bitcast(I32).rearrange("p (c e u) -> p c u e", e=2, u=2),
             m2[:].rearrange("p u v s -> p (u v s)").bitcast(I32).rearrange("p (u c e) -> p c u e", e=2, u=2),
         )
-        for step in range(1, len(steps)):
-            weave(steps[step][1][:], woven[step][:])
-            finish(step - 1)
-        finish(len(steps) - 1)
+        finish(1, woven0, 0, V)
+        weave(0)
+        finish(2, woven2, 0, V)
+        weave(1)
+        finish(3, woven1[0], *PIECES[0])
+        weave(2)
+        finish(3, woven1[1], *PIECES[1])
+        finish(3, woven1[2], *PIECES[2])

@@ -22,6 +22,7 @@ PACK = 4
 GROUP = 16
 ROW = 2 * V
 CHUNKS = ((0, 128), (128, 256), (256, 384), (384, 512))
+SHARE = 384
 PIECES = ((0, 256), (256, 384), (384, 512))
 
 
@@ -136,12 +137,15 @@ def tile_picked_yfmm_tanh_p_kernel(
                     stop=(d == D - 1),
                 )
 
-        m0 = last.tile([P, PACK, V], F32, name="m0", offset=8 * V - 64, align_bytes=64)
+        m0 = [
+            last.tile([P, PACK, V // 2], F32, name="m0_first", offset=8 * V - 64, align_bytes=64),
+            keep.tile([P, PACK, V // 2], F32, name="m0_second", align_bytes=64),
+        ]
         m1 = keep.tile([P, PACK, V], F32, name="m1", align_bytes=64)
         m2 = keep.tile([P, 2, V, 2], BF16, name="m2", align_bytes=64)
 
         def fetch(m, far, t, lo, hi, to_end=True):
-            nc.scalar.activation(m[:, t, lo:hi], window(t, to_end).indirect(entries(far, lo, hi)), COPY)
+            nc.scalar.activation(m, window(t, to_end).indirect(entries(far, lo, hi)), COPY)
 
         for t in range(PACK):
             pieces = PIECES if t == 0 else ((0, V),)
@@ -153,37 +157,40 @@ def tile_picked_yfmm_tanh_p_kernel(
                 else:
                     nc.vector.tensor_copy(h[:, t * ROW + lo : t * ROW + hi], bank[:])
             if t == 0:
-                fetch(m0, far1_sb, 0, 0, V // 2, False)
+                fetch(m0[0][:, 0, :], far1_sb, 0, 0, V // 2, False)
                 nc.vector.tensor_copy(m2[:, 0, :, 0], window(0, False).indirect(far3_sb[:]))
-        fetch(m0, far1_sb, 0, V // 2, V, False)
+        fetch(m0[1][:, 0, :], far1_sb, 0, V // 2, V, False)
         for t in (1, 2):
-            fetch(m0, far1_sb, t, 0, V // 2, False)
+            fetch(m0[0][:, t, :], far1_sb, t, 0, V // 2, False)
         for t in (1, 2, 3):
-            fetch(m0, far1_sb, t, V // 2, V)
-        fetch(m1, far2_sb, 0, 0, V)
-        fetch(m1, far2_sb, 1, 0, V)
-        for lo, hi in PIECES:
+            fetch(m0[1][:, t, :], far1_sb, t, V // 2, V)
+        for t in range(PACK):
+            fetch(m1[:, t, : V // 2], far2_sb, t, 0, V // 2)
+        for t in (0, 1):
+            fetch(m1[:, t, V // 2 :], far2_sb, t, V // 2, V)
+        for lo, hi in PIECES[1:]:
             for t in (2, 3):
-                fetch(m1, far2_sb, t, lo, hi)
+                fetch(m1[:, t, lo:hi], far2_sb, t, lo, hi)
 
         close_second = mid.tile([P, V // 2], U32, name="close_second", offset=0, align_bytes=64)
         nc.vector.tensor_copy(close_second[:], x_table[:].bitcast(U32).indirect(entries(close_sb, V // 2, V)))
         close_words = [close_first, close_second]
-        nc.vector.tensor_copy(m0[:, 3, : V // 2], window(3, True).indirect(entries(far1_sb, 0, V // 2)))
+        nc.vector.tensor_copy(m0[0][:, 3, :], window(3, True).indirect(entries(far1_sb, 0, V // 2)))
         for t in range(1, PACK):
             nc.vector.tensor_copy(m2[:, t // 2, :, t % 2], window(t, True).indirect(far3_sb[:]))
 
         small_bf = keep.tile([P, 4, N, PACK], BF16, name="small_bf", align_bytes=64)
         for i in range(4):
             nc.gpsimd.tensor_scalar(small_bf[:, i], small_raw[i][:].rearrange("p j n -> p n j"), 1.0, 0.0, MULT, ADD)
-        woven0 = early.tile([P, V, PACK], BF16, name="woven0", offset=64 + 12 * V, align_bytes=64)
-        for lo, hi in ((0, V // 2), (V // 2, V)):
-            nc.gpsimd.tensor_scalar(woven0[:, lo:hi, :], m0[:, :, lo:hi].rearrange("p t v -> p v t"), 1.0, 0.0, MULT, ADD)
+        woven0 = early.tile([P, SHARE, PACK], BF16, name="woven0", offset=64 + 12 * V, align_bytes=64)
+        for (lo, hi), part in zip(PIECES[:2], (m0[0][:], m0[1][:, :, :P])):
+            nc.gpsimd.tensor_scalar(woven0[:, lo:hi, :], part.rearrange("p t v -> p v t"), 1.0, 0.0, MULT, ADD)
 
         woven2 = last.tile([P, V, PACK], BF16, name="woven2", offset=0, align_bytes=64)
         small_scales = last.tile([P, V], U8, name="small_scales", offset=8 * V, align_bytes=64)
+        woven0_rest = last.tile([P, V - SHARE, PACK], BF16, name="woven0_rest", offset=9 * V, align_bytes=64)
         woven1 = [
-            last.tile([P, hi - lo, PACK], BF16, name="woven1_%d" % lo, offset=9 * V + 8 * lo, align_bytes=64)
+            last.tile([P, hi - lo, PACK], BF16, name="woven1_%d" % lo, offset=(13 * V, 11 * V, 17 * V)[PIECES.index((lo, hi))], align_bytes=64)
             for lo, hi in PIECES
         ]
 
@@ -225,9 +232,13 @@ def tile_picked_yfmm_tanh_p_kernel(
             woven2[:].rearrange("p v t -> p (v t)").bitcast(I32).rearrange("p (c e u) -> p c u e", e=2, u=2),
             m2[:].rearrange("p u v s -> p (u v s)").bitcast(I32).rearrange("p (u c e) -> p c u e", e=2, u=2),
         )
-        finish(1, woven0, 0, V)
-        weave(0)
+        finish(1, woven0, 0, SHARE)
+        nc.vector.tensor_copy(
+            woven0_rest[:].rearrange("p (c e) t -> p c t e", e=2), m0[1][:, :, P:].rearrange("p t (c e) -> p c t e", e=2)
+        )
         finish(2, woven2, 0, V)
+        weave(0)
+        finish(1, woven0_rest, SHARE, V)
         weave(1)
         finish(3, woven1[0], *PIECES[0])
         weave(2)

@@ -89,8 +89,8 @@ def tile_picked_yfmm_tanh_p_kernel(
         nc.vector.tensor_copy(pick_bytes.rearrange("p (d v) -> p v d", d=D), x_bytes[:].indirect(offs_sb[:]))
         pair_words = keep.tile([P, D, V], U32, name="pair_words", align_bytes=64)
         nc.vector.tensor_copy(pair_words[:].rearrange("p d v -> p v d"), x_table[:].bitcast(U32).indirect(offs_sb[:]))
-        close_first = keep.tile([P, V // 2], U32, name="close_first", align_bytes=64)
-        nc.vector.tensor_copy(close_first[:], x_table[:].bitcast(U32).indirect(entries(close_sb, 0, V // 2)))
+        close_first = keep.tile([P, SHARE], U32, name="close_first", align_bytes=64)
+        nc.vector.tensor_copy(close_first[:], x_table[:].bitcast(U32).indirect(entries(close_sb, 0, SHARE)))
 
         def place_rows(dst, src, first, queue):
             for r in range(4):
@@ -172,9 +172,9 @@ def tile_picked_yfmm_tanh_p_kernel(
             for t in (2, 3):
                 fetch(m1[:, t, lo:hi], far2_sb, t, lo, hi)
 
-        close_second = mid.tile([P, V // 2], U32, name="close_second", offset=0, align_bytes=64)
-        nc.vector.tensor_copy(close_second[:], x_table[:].bitcast(U32).indirect(entries(close_sb, V // 2, V)))
-        close_words = [close_first, close_second]
+        close_second = mid.tile([P, V - SHARE], U32, name="close_second", offset=0, align_bytes=64)
+        nc.vector.tensor_copy(close_second[:], x_table[:].bitcast(U32).indirect(entries(close_sb, SHARE, V)))
+        close_words = [close_first[:, lo:hi] for lo, hi in CHUNKS[:3]] + [close_second[:]]
         nc.vector.tensor_copy(m0[0][:, 3, :], window(3, True).indirect(entries(far1_sb, 0, V // 2)))
         for t in range(1, PACK):
             nc.vector.tensor_copy(m2[:, t // 2, :, t % 2], window(t, True).indirect(far3_sb[:]))
@@ -211,7 +211,7 @@ def tile_picked_yfmm_tanh_p_kernel(
             )
 
         for c, (lo, hi) in enumerate(CHUNKS):
-            product(0, c, close_words[c // 2][:, lo % 256 : lo % 256 + hi - lo], close_bytes[:, lo:hi])
+            product(0, c, close_words[c], close_bytes[:, lo:hi])
 
         def finish(i, woven, lo, hi):
             codes, scales = quantize(woven[:].rearrange("p c t -> p (c t)"), "m%d_%d" % (i, lo))

@@ -20,9 +20,10 @@ ADD = mybir.AluOpType.add
 P = 128
 PACK = 4
 GROUP = 16
-ROW = 2 * V
+ROW = V + 192
 CHUNKS = ((0, 128), (128, 256), (256, 384), (384, 512))
 SHARE = 384
+FIRST = 320
 PIECES = ((0, 256), (256, 384), (384, 512))
 
 
@@ -60,7 +61,7 @@ def tile_picked_yfmm_tanh_p_kernel(
             x_bytes[0:32, :].bitcast(I32), x_scales[0].bitcast(I32).unsqueeze(1).to_broadcast([16, 2, T // 4])
         )
         nc.vector.memset(x_bytes[32:64, :].bitcast(I32), 0)
-        nc.vector.memset(x_bytes[64:P, :].bitcast(I32), 0)
+        nc.gpsimd.memset(x_bytes[64:P, :].bitcast(I32), 0)
         offs_sb = load_list(offs, "offs_sb")
         close_sb = load_list(close, "close_sb")
         far1_sb = load_list(far1, "far1_sb")
@@ -138,8 +139,8 @@ def tile_picked_yfmm_tanh_p_kernel(
                 )
 
         m0 = [
-            last.tile([P, PACK, V // 2], F32, name="m0_first", offset=8 * V - 64, align_bytes=64),
-            keep.tile([P, PACK, V // 2], F32, name="m0_second", align_bytes=64),
+            last.tile([P, PACK, FIRST], F32, name="m0_first", offset=8 * V - 64, align_bytes=64),
+            keep.tile([P, PACK, V - FIRST], F32, name="m0_second", align_bytes=64),
         ]
         m1 = keep.tile([P, PACK, V], F32, name="m1", align_bytes=64)
         m2 = keep.tile([P, 2, V, 2], BF16, name="m2", align_bytes=64)
@@ -157,13 +158,13 @@ def tile_picked_yfmm_tanh_p_kernel(
                 else:
                     nc.vector.tensor_copy(h[:, t * ROW + lo : t * ROW + hi], bank[:])
             if t == 0:
-                fetch(m0[0][:, 0, :], far1_sb, 0, 0, V // 2, False)
+                fetch(m0[0][:, 0, :], far1_sb, 0, 0, FIRST, False)
                 nc.vector.tensor_copy(m2[:, 0, :, 0], window(0, False).indirect(far3_sb[:]))
-        fetch(m0[1][:, 0, :], far1_sb, 0, V // 2, V, False)
+        fetch(m0[1][:, 0, :], far1_sb, 0, FIRST, V, False)
         for t in (1, 2):
-            fetch(m0[0][:, t, :], far1_sb, t, 0, V // 2, False)
+            fetch(m0[0][:, t, :], far1_sb, t, 0, FIRST, False)
         for t in (1, 2, 3):
-            fetch(m0[1][:, t, :], far1_sb, t, V // 2, V)
+            fetch(m0[1][:, t, :], far1_sb, t, FIRST, V)
         for t in range(PACK):
             fetch(m1[:, t, : V // 2], far2_sb, t, 0, V // 2)
         for t in (0, 1):
@@ -175,7 +176,7 @@ def tile_picked_yfmm_tanh_p_kernel(
         close_second = mid.tile([P, V - SHARE], U32, name="close_second", offset=0, align_bytes=64)
         nc.vector.tensor_copy(close_second[:], x_table[:].bitcast(U32).indirect(entries(close_sb, SHARE, V)))
         close_words = [close_first[:, lo:hi] for lo, hi in CHUNKS[:3]] + [close_second[:]]
-        nc.vector.tensor_copy(m0[0][:, 3, :], window(3, True).indirect(entries(far1_sb, 0, V // 2)))
+        nc.vector.tensor_copy(m0[0][:, 3, :], window(3, True).indirect(entries(far1_sb, 0, FIRST)))
         for t in range(1, PACK):
             nc.vector.tensor_copy(m2[:, t // 2, :, t % 2], window(t, True).indirect(far3_sb[:]))
 
@@ -183,7 +184,7 @@ def tile_picked_yfmm_tanh_p_kernel(
         for i in range(4):
             nc.gpsimd.tensor_scalar(small_bf[:, i], small_raw[i][:].rearrange("p j n -> p n j"), 1.0, 0.0, MULT, ADD)
         woven0 = early.tile([P, SHARE, PACK], BF16, name="woven0", offset=64 + 12 * V, align_bytes=64)
-        for (lo, hi), part in zip(PIECES[:2], (m0[0][:], m0[1][:, :, :P])):
+        for (lo, hi), part in zip(((0, FIRST), (FIRST, SHARE)), (m0[0][:], m0[1][:, :, : SHARE - FIRST])):
             nc.gpsimd.tensor_scalar(woven0[:, lo:hi, :], part.rearrange("p t v -> p v t"), 1.0, 0.0, MULT, ADD)
 
         woven2 = last.tile([P, V, PACK], BF16, name="woven2", offset=0, align_bytes=64)
@@ -234,7 +235,7 @@ def tile_picked_yfmm_tanh_p_kernel(
         )
         finish(1, woven0, 0, SHARE)
         nc.vector.tensor_copy(
-            woven0_rest[:].rearrange("p (c e) t -> p c t e", e=2), m0[1][:, :, P:].rearrange("p t (c e) -> p c t e", e=2)
+            woven0_rest[:].rearrange("p (c e) t -> p c t e", e=2), m0[1][:, :, SHARE - FIRST :].rearrange("p t (c e) -> p c t e", e=2)
         )
         finish(2, woven2, 0, V)
         weave(0)

from contextlib import ExitStack

import concourse.mybir as mybir

K, T, S, D, H, N, V = 512, 2048, 1024, 2, 512, 128, 512
FLOPS = 2 * K * H * S + 3 * 2 * H * N * V + 2 * K * N * V

F32 = mybir.dt.float32
BF16 = mybir.dt.bfloat16
I32 = mybir.dt.int32
U32 = mybir.dt.uint32
U16 = mybir.dt.uint16
U8 = mybir.dt.uint8
FP8X4 = mybir.dt.float8_e4m3fn_x4
TANH = mybir.ActivationFunctionType.Tanh
COPY = mybir.ActivationFunctionType.Copy
MULT = mybir.AluOpType.mult
ADD = mybir.AluOpType.add

P = 128
PACK = 4
GROUP = 16
ROW = V + 192
CHUNKS = ((0, 128), (128, 256), (256, 384), (384, 512))
SHARE = 384
FIRST = 320
PIECES = ((0, 256), (256, 384), (384, 512))


def tile_picked_yfmm_tanh_p_kernel(
    tc, x_words, x_scales, w1, t1, t2, t3, w2, bias, offs, far1, far2, far3, close, out
):
    nc = tc.nc
    with ExitStack() as ctx:
        keep = ctx.enter_context(tc.tile_pool(name="keep", bufs=1))
        late = ctx.enter_context(tc.tile_pool(name="late", bufs=1))
        early = ctx.enter_context(tc.tile_pool(name="early", bufs=1))
        mid = ctx.enter_context(tc.tile_pool(name="mid", bufs=1))
        last = ctx.enter_context(tc.tile_pool(name="last", bufs=1))
        psum = ctx.enter_context(tc.psum_pool(name="psum", bufs=1))

        def load_list(src, name):
            tile = keep.tile(list(src.shape), U16, name=name)
            nc.sync.dma_start(tile[:], src)
            return tile

        def entries(tile, lo, hi):
            return tile[:, lo // GROUP : hi // GROUP]

        def quantize(values, name, codes=None, scales=None):
            width = values.shape[1] // PACK
            if codes is None:
                codes = keep.tile([P, width], U32, name=name + "_codes", align_bytes=64)
            if scales is None:
                scales = keep.tile([P, width], U8, name=name + "_scales", align_bytes=64)
            nc.vector.quantize_mx(out=codes[:].bitcast(FP8X4), scales=scales[:], in_=values)
            return codes, scales

        x_bytes = keep.tile([P, T], U8, name="x_bytes", align_bytes=64)
        nc.sync.dma_start(
            x_bytes[0:32, :].bitcast(I32), x_scales[0].bitcast(I32).unsqueeze(1).to_broadcast([16, 2, T // 4])
        )
        nc.vector.memset(x_bytes[32:64, :].bitcast(I32), 0)
        nc.gpsimd.memset(x_bytes[64:P, :].bitcast(I32), 0)
        offs_sb = load_list(offs, "offs_sb")
        close_sb = load_list(close, "close_sb")
        far1_sb = load_list(far1, "far1_sb")
        x_table = keep.tile([P, T], I32, name="x_table", align_bytes=64)
        nc.sync.dma_start(x_table[:], x_words[0].rearrange("p c r -> p (c r)").bitcast(I32))
        w1_rows = w1.rearrange("(p j) c -> p j c", j=PACK)
        w1_raw = [
            keep.tile([P, PACK, H // 2], F32, name="w1_raw0"),
            late.tile([P, PACK, H // 2], F32, name="w1_raw1", offset=0, align_bytes=64),
        ]
        for half in range(2):
            nc.sync.dma_start(w1_raw[half][:], w1_rows[:, :, half * (H // 2) : (half + 1) * (H // 2)])
        far2_sb = load_list(far2, "far2_sb")
        far3_sb = load_list(far3, "far3_sb")

        h = keep.tile([P, PACK * ROW], F32, name="h", align_bytes=64)
        nc.vector.memset(h[:, V:ROW], 0.0)
        for t in range(1, PACK):
            nc.scalar.activation(h[:, t * ROW + V : (t + 1) * ROW], h[:, V:ROW], COPY)

        def window(t, to_end):
            return h[:, t * ROW : (PACK if to_end else t + 1) * ROW]

        pick_tile = early.tile([P, 64 + 16 * V], U8, name="pick_bytes", offset=0, align_bytes=64)
        pick_bytes = pick_tile[:, :S]
        nc.vector.tensor_copy(pick_bytes.rearrange("p (d v) -> p v d", d=D), x_bytes[:].indirect(offs_sb[:]))
        pair_words = keep.tile([P, D, V], U32, name="pair_words", align_bytes=64)
        nc.vector.tensor_copy(pair_words[:].rearrange("p d v -> p v d"), x_table[:].bitcast(U32).indirect(offs_sb[:]))
        close_first = keep.tile([P, SHARE], U32, name="close_first", align_bytes=64)
        nc.vector.tensor_copy(close_first[:], x_table[:].bitcast(U32).indirect(entries(close_sb, 0, SHARE)))

        def place_rows(dst, src, first, queue):
            for r in range(4):
                queue.dma_start(dst[r:P:32, :].bitcast(I32), src[2 * r + first : 32 : 8, :].bitcast(I32))

        pair_flat = keep.tile([P, S], U8, name="pair_bytes", align_bytes=64)
        place_rows(pair_flat, pick_bytes, 0, nc.scalar)
        pair_bytes = pair_flat[:].rearrange("p (d v) -> p d v", d=D)

        small_raw = []
        for i, mat in enumerate((w2, t1, t3, t2)):
            raw = early.tile([P, PACK, N], F32, name="small_raw%d" % i, offset=64 + 4 * V * i, align_bytes=64)
            nc.sync.dma_start(raw[:], mat.rearrange("(p j) n -> p j n", j=PACK))
            small_raw.append(raw)
        bias_sb = early.tile([P, 1], F32, name="bias_sb", offset=0, align_bytes=64)
        nc.sync.dma_start(bias_sb[:], bias)

        w1_bf = [keep.tile([P, 2, P, PACK], BF16, name="w1_bf%d" % u, align_bytes=64) for u in range(2)]
        for half in range(2):
            ms = slice(half * (P // 2), (half + 1) * (P // 2))
            src = w1_raw[half][:].rearrange("p j (m t) -> p m j t", t=PACK)
            for u in range(2):
                nc.scalar.copy(w1_bf[u][:, :, ms, :].rearrange("p t m j -> p m j t"), src[:, :, :, 2 * u : 2 * u + 2])
        w1_mx = [quantize(w1_bf[0][:, t].rearrange("p m j -> p (m j)"), "w1_%d" % t) for t in range(2)]
        codes = mid.tile([P, 2 * P], U32, name="w1_23_codes", offset=0, align_bytes=64)
        codes, scales = quantize(w1_bf[1][:].rearrange("p t m j -> p (t m j)"), "w1_23", codes=codes)
        for t in range(2):
            w1_mx.append((codes[:, t * P : (t + 1) * P], scales[:, t * P : (t + 1) * P]))

        close_picked = late.tile([P, V], U8, name="close_picked", offset=0, align_bytes=64)
        nc.vector.tensor_copy(close_picked[:], x_bytes[:].indirect(close_sb[:]))
        close_bytes = keep.tile([P, V], U8, name="close_bytes", align_bytes=64)
        place_rows(close_bytes, close_picked, 1, nc.sync)

        def moments(t, bank, lo, hi):
            for d in range(D):
                nc.tensor.matmul_mx(
                    out=bank,
                    lhsT=w1_mx[t][0][:, :].bitcast(FP8X4),
                    lhsT_scale=w1_mx[t][1][:, :],
                    rhs=pair_words[:, d, lo:hi].bitcast(FP8X4),
                    rhs_scale=pair_bytes[:, d, lo:hi],
                    start=(d == 0),
                    stop=(d == D - 1),
                )

        m0 = [
            last.tile([P, PACK, FIRST], F32, name="m0_first", offset=8 * V - 64, align_bytes=64),
            keep.tile([P, PACK, V - FIRST], F32, name="m0_second", align_bytes=64),
        ]
        m1 = keep.tile([P, PACK, V], F32, name="m1", align_bytes=64)
        m2 = keep.tile([P, 2, V, 2], BF16, name="m2", align_bytes=64)

        def fetch(m, far, t, lo, hi, to_end=True):
            nc.scalar.activation(m, window(t, to_end).indirect(entries(far, lo, hi)), COPY)

        for t in range(PACK):
            pieces = PIECES if t == 0 else ((0, V),)
            for i, (lo, hi) in enumerate(pieces):
                bank = psum.tile([P, hi - lo], F32, name="h_bank", tag="bank%d" % (i if t == 0 else (1, 3, 4)[t - 1]))
                moments(t, bank[:], lo, hi)
                if t < 2:
                    nc.scalar.copy(h[:, t * ROW + lo : t * ROW + hi], bank[:])
                else:
                    nc.vector.tensor_copy(h[:, t * ROW + lo : t * ROW + hi], bank[:])
            if t == 0:
                fetch(m0[0][:, 0, :], far1_sb, 0, 0, FIRST, False)
                nc.vector.tensor_copy(m2[:, 0, :, 0], window(0, False).indirect(far3_sb[:]))
        fetch(m0[1][:, 0, :], far1_sb, 0, FIRST, V, False)
        for t in (1, 2):
            fetch(m0[0][:, t, :], far1_sb, t, 0, FIRST, False)
        for t in (1, 2, 3):
            fetch(m0[1][:, t, :], far1_sb, t, FIRST, V)
        for t in range(PACK):
            fetch(m1[:, t, : V // 2], far2_sb, t, 0, V // 2)
        for t in (0, 1):
            fetch(m1[:, t, V // 2 :], far2_sb, t, V // 2, V)
        for lo, hi in PIECES[1:]:
            for t in (2, 3):
                fetch(m1[:, t, lo:hi], far2_sb, t, lo, hi)

        close_second = mid.tile([P, V - SHARE], U32, name="close_second", offset=0, align_bytes=64)
        nc.vector.tensor_copy(close_second[:], x_table[:].bitcast(U32).indirect(entries(close_sb, SHARE, V)))
        close_words = [close_first[:, lo:hi] for lo, hi in CHUNKS[:3]] + [close_second[:]]
        nc.vector.tensor_copy(m0[0][:, 3, :], window(3, True).indirect(entries(far1_sb, 0, FIRST)))
        for t in range(1, PACK):
            nc.vector.tensor_copy(m2[:, t // 2, :, t % 2], window(t, True).indirect(far3_sb[:]))

        small_bf = keep.tile([P, 4, N, PACK], BF16, name="small_bf", align_bytes=64)
        for i in range(4):
            nc.gpsimd.tensor_scalar(small_bf[:, i], small_raw[i][:].rearrange("p j n -> p n j"), 1.0, 0.0, MULT, ADD)
        woven0 = early.tile([P, SHARE, PACK], BF16, name="woven0", offset=64 + 12 * V, align_bytes=64)
        for (lo, hi), part in zip(((0, FIRST), (FIRST, SHARE)), (m0[0][:], m0[1][:, :, : SHARE - FIRST])):
            nc.gpsimd.tensor_scalar(woven0[:, lo:hi, :], part.rearrange("p t v -> p v t"), 1.0, 0.0, MULT, ADD)

        woven2 = last.tile([P, V, PACK], BF16, name="woven2", offset=0, align_bytes=64)
        small_scales = last.tile([P, V], U8, name="small_scales", offset=8 * V, align_bytes=64)
        woven0_rest = last.tile([P, V - SHARE, PACK], BF16, name="woven0_rest", offset=9 * V, align_bytes=64)
        woven1 = [
            last.tile([P, hi - lo, PACK], BF16, name="woven1_%d" % lo, offset=(13 * V, 11 * V, 17 * V)[PIECES.index((lo, hi))], align_bytes=64)
            for lo, hi in PIECES
        ]

        codes, scales = quantize(small_bf[:].rearrange("p i n j -> p (i n j)"), "small", scales=small_scales)
        small = [(codes[:, i * N : (i + 1) * N], scales[:, i * N : (i + 1) * N]) for i in range(4)]

        banks = [psum.tile([P, hi - lo], F32, name="out_bank%d" % c, tag="bank%d" % c) for c, (lo, hi) in enumerate(CHUNKS)]

        def product(i, c, codes, scales):
            nc.tensor.matmul_mx(
                out=banks[c][:],
                lhsT=small[i][0].bitcast(FP8X4),
                lhsT_scale=small[i][1],
                rhs=codes.bitcast(FP8X4),
                rhs_scale=scales,
                start=(i == 0),
                stop=(i == 3),
            )

        for c, (lo, hi) in enumerate(CHUNKS):
            product(0, c, close_words[c], close_bytes[:, lo:hi])

        def finish(i, woven, lo, hi):
            codes, scales = quantize(woven[:].rearrange("p c t -> p (c t)"), "m%d_%d" % (i, lo))
            for c, (a, b) in enumerate(CHUNKS):
                if lo <= a and b <= hi:
                    product(i, c, codes[:, a - lo : b - lo], scales[:, a - lo : b - lo])
                    if i == 3:
                        result = keep.tile([P, b - a], F32, name="result%d" % c)
                        nc.scalar.activation(result[:], banks[c][:], TANH, bias=bias_sb[:])
                        nc.sync.dma_start(out[:, a:b], result[:])

        def weave(k):
            nc.vector.tensor_copy(
                woven1[k][:].rearrange("p (c e) t -> p c t e", e=2), m1[:, :, PIECES[k][0] : PIECES[k][1]].rearrange("p t (c e) -> p c t e", e=2)
            )

        nc.vector.tensor_copy(
            woven2[:].rearrange("p v t -> p (v t)").bitcast(I32).rearrange("p (c e u) -> p c u e", e=2, u=2),
            m2[:].rearrange("p u v s -> p (u v s)").bitcast(I32).rearrange("p (u c e) -> p c u e", e=2, u=2),
        )
        finish(1, woven0, 0, SHARE)
        nc.vector.tensor_copy(
            woven0_rest[:].rearrange("p (c e) t -> p c t e", e=2), m0[1][:, :, SHARE - FIRST :].rearrange("p t (c e) -> p c t e", e=2)
        )
        finish(2, woven2, 0, V)
        weave(0)
        finish(1, woven0_rest, SHARE, V)
        weave(1)
        finish(3, woven1[0], *PIECES[0])
        weave(2)
        finish(3, woven1[1], *PIECES[1])
        finish(3, woven1[2], *PIECES[2])
